import numpy as np, ml_dtypes
CORES = [40,41,42,43,44,45,46,47]
N = 8
BF = ml_dtypes.bfloat16
def gentries(a):
    return np.ascontiguousarray(a.reshape(8, 16, -1).transpose(0, 2, 1)).reshape(8, -1)
def gtable(e):
    e = np.asarray(e); return np.ascontiguousarray(e.reshape(8, -1, 16).transpose(0, 2, 1)).reshape(128, -1).astype(np.int32)
V, D, B, C = 1024, 6, 128, 256
NONE = 1 << 24
def ring(n, s, order, step):
    n[order, s] = np.roll(order, -step); n[order, s + 1] = np.roll(order, step)
def mesh(rng, pairs):
    n = np.zeros((N * V, D), np.int64); h = D // 2 - 1
    if pairs:
        q = rng.permutation(N)
        circles = [np.stack([q[i] * V + rng.permutation(B), q[i + 1] * V + rng.permutation(B)], 1).reshape(-1) for i in range(0, N, 2)]
    else:
        circles = [rng.permutation((np.arange(N)[:, None] * V + np.arange(B)).reshape(-1))]
    for o in circles:
        for i in range(h): ring(n, 2 * i, o, 2 * i + 1)
    for r in range(N):
        a = r * V + rng.permutation(B); m = r * V + B + rng.permutation(B); p = r * V + C + rng.permutation(V - C)
        ring(n, 2 * h, np.stack([a, m], 1).reshape(-1), 1)
        at = np.zeros(V - B, bool); at[rng.permutation(V - B)[:B]] = True
        o = np.zeros(V - B, np.int64); o[at] = rng.permutation(m); o[~at] = p
        for i in range(h): ring(n, 2 * i, o, i + 1)
        ring(n, 2 * h, p, h + 1)
    return rng.permuted(n, axis=1)
def planes(rng, *shape):
    p = rng.integers(np.array([-3, -3, -3, -10]), np.array([4, 4, 4, 11]), shape + (3, 4))
    return np.matmul(p.swapaxes(-1, -2), p)
def parts(rng, pairs=False):
    return planes(rng, N, 8, V), rng.integers(-15, 16, (N, 8, V, 3)), np.stack([mesh(rng, pairs) for g in range(8)])
def pack(q, c, n):
    h = np.concatenate([c, np.ones(c.shape[:-1] + (1,), c.dtype)], -1); p = h[..., :, None] * h[..., None, :]
    e = n.reshape(8, N, V, D).transpose(1, 0, 3, 2).reshape(N, 8, D * V)
    return {"qu": np.ascontiguousarray(q.transpose(0, 1, 3, 4, 2)).reshape(N, 128, V).astype(np.float32),
            "po": np.ascontiguousarray(p.transpose(0, 1, 3, 4, 2)).reshape(N, 128, V).astype(np.float32).astype(BF),
            "nb": np.stack([gtable(e[r]) for r in range(N)])}
def setup_inputs(rng):
    return pack(*parts(rng))
def setup_inputs_ties(rng):
    n = parts(rng)[2]; G = np.arange(8)[None, :, None]
    a = planes(rng, 8, 2) + np.array([1, 2])[:, None, None] * np.eye(4, dtype=np.int64); b = rng.integers(-15, 16, (8, 2, 3))
    return pack(a[G, rng.integers(0, 2, (N, 8, V))], b[G, rng.integers(0, 2, (N, 8, V))], n)
def setup_inputs_stars(rng):
    q, c, n = parts(rng); c[..., 0] = np.minimum(c[..., 0], 14)
    for g in range(8):
        m = n[g]; v = rng.permutation((np.arange(N)[:, None] * V + np.arange(B)).reshape(-1)); k = m[v]
        meet = (m[k][:, :, :, None] == k[:, None, None, :]).any((1, 2, 3)); used = np.zeros(N * V, bool); done = 0
        for w in v[~meet]:
            leaf = m[w]; near = np.concatenate([leaf, m[leaf].reshape(-1)])
            if used[near].any(): continue
            used[near] = True; done += 1
            for u in np.append(leaf, w):
                q[u // V, g, u % V] = 0; q[u // V, g, u % V, 0, 3] = q[u // V, g, u % V, 3, 0] = -499; c[u // V, g, u % V, 0] = 15 if u == w else -15
            if done == 4: break
        assert done == 4
    return pack(q, c, n)
def setup_inputs_pairs(rng):
    return pack(*parts(rng, True))
def setup_inputs_heavy(rng):
    n = np.stack([mesh(rng, False) for g in range(8)]); G = np.arange(8)[None, :, None]
    x = rng.integers(0, 9, (N, 8, V, 4, 4)); k = np.tril(x) + np.tril(x, -1).swapaxes(-1, -2)
    s = np.where(G < 4, -1, np.where(G < 6, 1, 1 - 2 * rng.integers(0, 2, (N, 8, V))))
    d = pack(s[..., None, None] * (500 - k), rng.integers(12, 16, (N, 8, V, 3)), n)
    n_all = lists_of(d["nb"]); q_all = whole_meshes(d["qu"]); p_all = whole_meshes(d["po"]); own = np.arange(N * V); large = 0
    for g in range(4):
        m1 = collapse(costs(q_all[g], p_all[g], n_all[g]), n_all[g]); q1 = q_all[g].copy()
        for i in range(D): q1 += np.where(m1[n_all[g, i]] == own, q_all[g][:, n_all[g, i]], 0)
        n2 = m1[n_all[g]]; c2 = np.where(n2 == own, NONE, costs(q1, p_all[g], n2)); m2 = collapse(c2, n2)
        large += np.count_nonzero((m1 == own) & (m2 != own) & (np.min(c2, axis=0) < -(1 << 22)))
    assert large > 0
    return d
def setup_inputs_spread(rng):
    q, c, n = parts(rng); a = (500 >> rng.integers(0, 9, (N, 8, V)))[..., None, None]
    x = rng.integers(-a, a + 1, (N, 8, V, 4, 4)); x = np.where(rng.random((N, 8, V, 1, 1)) < 0.0625, 500 - 1000 * rng.integers(0, 2, x.shape), x)
    q = np.tril(x) + np.tril(x, -1).swapaxes(-1, -2); k = rng.integers(0, 8, c.shape)
    c = np.where(k == 0, 0, np.where(k == 1, 15, np.where(k == 2, -15, c)))
    return pack(q, c, n)
def lists_of(nb):
    return np.stack([gentries(nb[r]).reshape(8, D, V) for r in range(N)], axis=2).reshape(8, D, N * V).astype(np.int64)
def whole_meshes(x):
    return x.astype(np.float64).reshape(N, 8, 16, V).transpose(1, 2, 0, 3).reshape(8, 16, N * V).astype(np.int64)
def check_inputs(d):
    bad = []; q = d["qu"].astype(np.float64).reshape(N, 8, 4, 4, V); p = d["po"].astype(np.float64).reshape(N, 8, 4, 4, V); h = p[:, :, :, 3]
    if not np.isfinite(q).all() or (q != np.rint(q)).any() or (np.abs(q) > 500).any(): bad.append("quadrics: whole numbers of size at most 500")
    if (q != q.transpose(0, 1, 3, 2, 4)).any(): bad.append("quadrics: symmetric")
    if not np.isfinite(p).all() or (h != np.rint(h)).any() or (np.abs(h) > 15).any() or (h[:, :, 3] != 1).any() or (p != h[:, :, :, None] * h[:, :, None]).any(): bad.append("points: products of whole coordinates of size at most 15 and 1")
    n = lists_of(d["nb"]).transpose(0, 2, 1); own = np.arange(N * V)[None, :, None]
    if (n < 0).any() or (n >= N * V).any(): return bad + ["neighbours: in range"]
    s = np.sort(n, axis=2)
    if (n == own).any() or (s[:, :, 1:] == s[:, :, :-1]).any(): bad.append("neighbours: different, not the vertex itself")
    if (np.sort((own * (N * V) + n).reshape(8, -1), axis=1) != np.sort((n * (N * V) + own).reshape(8, -1), axis=1)).any(): bad.append("neighbours: symmetric")
    if ((own // V != n // V) & ((own % V >= B) | (n % V >= B))).any(): bad.append("edges between ranks: columns under B")
    if ((own % V < B) & (n % V >= C)).any(): bad.append("neighbours of columns under B: columns under C")
    return bad
def costs(q, p, n):
    return np.stack([np.sum((q + q[:, n[s]]) * p[:, n[s]], axis=0) for s in range(D)])
def collapse(cost, n):
    own = np.arange(N * V); s = np.argmin(cost, axis=0)
    best = cost[s, own]; first = (best < best[n]) | ((best == best[n]) & (own < n)) | (n == own)
    return np.where(np.all(first, axis=0) & (best < NONE), n[s, own], own)
def reference(qu, po, nb):
    n_all = lists_of(nb); q_all = whole_meshes(qu); p_all = whole_meshes(po); own = np.arange(N * V)
    q1 = q_all.copy(); goal = np.zeros((8, N * V), np.int64)
    for g in range(8):
        n = n_all[g]; q = q_all[g]; p = p_all[g]
        m1 = collapse(costs(q, p, n), n)
        for s in range(D): q1[g] += np.where(m1[n[s]] == own, q[:, n[s]], 0)
        n2 = m1[n]
        m2 = collapse(np.where(n2 == own, NONE, costs(q1[g], p, n2)), n2)
        goal[g] = m2[m1]
    q1 = np.ascontiguousarray(q1.reshape(8, 16, N, V).transpose(2, 0, 1, 3)).reshape(N, 128, V)
    goal = np.ascontiguousarray(goal.reshape(8, N, V).transpose(1, 0, 2))
    return {"q1": q1.astype(np.float32), "goal": goal.astype(np.float32)}

@@ -1,0 +1,503 @@
+from concourse.bass import DstId, RemoteDMATransfer
+from concourse.mybir import AluOpType, ActivationFunctionType
+
+A = AluOpType
+COPY = ActivationFunctionType.Copy
+IDENT = ActivationFunctionType.Identity
+NV = 1024
+CH = [(0, 2), (2, 3), (5, 3)]
+BIG = float(1 << 26)
+RESET = float(1 << 29)
+ZERO = 8192
+VS = {"A": (2, 2, 2), "D": (4, 3, 3), "E": (1, 1, 2)}
+PIECE = 6
+NEMAX = 48 * max(n for _c, n in CH)
+CYC, GAT, PEC, WAKE, DMAL, REML, FIRST, BW, LOOK, SHARE = 0.00104, 1.5, 0.00055, 0.08, 2.0, 3.6, 2.0, 200000.0, 0.12, 0.3
+PRI = {'W02V': -14.5, 'F02S': 1.0, 'A02V': 6.5, 'D02V': 3.5, 'E12V': -0.5, 'B01V': 9.5, 'A12V': -17.5, 'E12S': 42.0, 'W01V': 11.0,
+       'G21V': -2.0, 'W22V': 4.5, 'A22S': -6.0, 'E01V': -2.0, 'F12V': -12.0, '021V': 1.0, 'A11S': -5.5, 'B22V': 2.5, 'E22V': -1.5,
+       'W22S': -7.0, 'W12V': -3.0, 'W21V': 2.5, 'D22S': 13.0, 'W11V': -1.0, 'F11V': -4.0, '011V': 5.0, 'D22V': -8.5, 'E01S': -3.5,
+       '021S': -11.5, 'D12S': 29.0, 'A21S': 5.5, 'D12V': -20.0, 'C02V': 20.0, 'D01S': -5.5, 'F01V': 8.5, 'A01S': 0.5, 'E21S': -19.5,
+       'F02V': 7.0, 'W12S': -4.5, 'A22V': -9.0, 'C12S': -5.5, '001S': -8.5, 'A01V': 1.5, 'C12V': -22.0, 'A02S': 18.0, 'F21V': 10.0,
+       'C02S': 6.0, 'G22V': 20.5, 'W01S': -23.5, 'D21S': -4, 'W02S': 19.5, 'A12S': -2.0, 'G22S': 14.5, 'B02V': 35.5, 'F12S': -3.0,
+       'C22S': 0.5, 'E22S': 9.0, 'B12V': 6.5, 'E02V': -10.0, 'F22V': 1.5, 'W11S': -11.0, 'C01V': 28.5, 'E02S': 25.5, 'B12S': 2.0,
+       'D02S': 8.5, 'G21S': 4.0, 'B22S': -13.0, '001V': 2.0, 'F22S': 1.5, 'D11S': 1.0, 'W21S': -20.0, 'B02S': 12.5, 'E11S': -0.5,
+       'C22V': 5.0, 'D21V': -1}
+
+SCRATCH = {"nb3": ("sbuf", [128, 6, 64], "int32"), "ci": ("sbuf", [128, 8], "int32")}
+for _names, _cols, _dt in [
+        ("W1 W2 WB WC", 8192, "bfloat16"), ("WG", 8192, "float32"), ("QW", 8200, "float32"),
+        ("PR", 6144, "float32"), ("GD", 4096, "float32"), ("GA GB", 6144, "bfloat16"),
+        ("Pn", 1024, "bfloat16"), ("Qs acc", 1024, "float32"),
+        ("off1 offD offE", 384, "uint16"), ("offG", 64, "uint16"), ("nbz vL xL", 384, "float32"),
+        ("vT Er Mn kp ids dl sc sd", 384, "float32"), ("tz", 768, "bfloat16"), ("t2 ab", 384, "bfloat16"),
+        ("Es dch tm tn to", 64, "float32"),
+        ("patR patK", NEMAX, "float32"), ("cf gi RA", 16, "float32"), ("RE", 8, "float32"), ("RB", 16, "bfloat16"),
+        ("ones idn dbl bigi", 128, "bfloat16"), ("idf", 128, "float32"), ("sel", 144, "bfloat16")]:
+    for _x in _names.split():
+        SCRATCH[_x] = ("sbuf", [128, _cols], _dt)
+for _k, (_c, _n) in enumerate(CH):
+    SCRATCH["X1%d" % _k] = ("sbuf", [128, 8, 16 * _n], "bfloat16")
+    SCRATCH["X2%d" % _k] = ("sbuf", [128, 8, 16 * _n], "bfloat16")
+    SCRATCH["qk%d" % _k] = ("psum", [128, 512], "float32")
+    SCRATCH["tk%d" % _k] = ("psum", [128, 512], "float32")
+SCRATCH["wa0"] = ("psum", [128, 512], "float32")
+SCRATCH["wa1"] = ("psum", [128, 512], "float32")
+
+SENDS = ["Q", "W1", "WB", "WC", "W2", "WF", "WG"]
+SEMAPHORES = (["cV", "cS", "cP", "cG", "dnb", "dgo"] + ["dq%d" % k for k in range(4)] + ["dp%d" % k for k in range(4)]
+              + ["do%d" % k for k in range(3)] + ["df%d" % k for k in range(6)] + ["a" + x for x in SENDS] + ["l" + x for x in SENDS])
+
+
+def arrange(ops):
+    n = len(ops)
+    writer, readers = {}, {}
+    pred = [set() for _ in ops]
+    for i, o in enumerate(ops):
+        for k in o["r"]:
+            if k in writer:
+                pred[i].add(writer[k])
+        for k in o["w"]:
+            if k in writer:
+                pred[i].add(writer[k])
+            pred[i].update(readers.get(k, ()))
+        pred[i].discard(i)
+        for k in o["r"]:
+            readers.setdefault(k, set()).add(i)
+        for k in o["w"]:
+            writer[k] = i
+            readers[k] = set()
+    succ = [[] for _ in ops]
+    for i in range(n):
+        for j in pred[i]:
+            succ[j].append(i)
+    tail = [0.0] * n
+    for i in range(n - 1, -1, -1):
+        o = ops[i]
+        tail[i] = o["alt"][0][3] + o["lat"] + o["bytes"] / BW + WAKE + max([tail[j] for j in succ[i]] + [0.0]) + o["bump"]
+    left = [len(p) for p in pred]
+    ready = [i for i in range(n) if not left[i]]
+    done, who = [0.0] * n, [None] * n
+    free, bank, dma, first = {}, {}, [0.0], [FIRST]
+    order = []
+
+    def start(i, q):
+        t = free.get(q, 0.0)
+        for j in pred[i]:
+            t = max(t, done[j] + (0.0 if q == "P" and who[j] == "P" else WAKE))
+        for b in ops[i]["banks"]:
+            for q2, t2 in bank.get(b, {}).items():
+                if q2 != q:
+                    t = max(t, t2 + WAKE)
+        return t
+    while ready:
+        cand = [(start(i, a[0]), i, a) for i in ready for a in ops[i]["alt"]]
+        st = {(i, a[0]): t for t, i, a in cand}
+        cand = [c for c in cand if not (c[2][0] == "V" and st.get((c[1], "S"), 1e9) <= c[0] + SHARE)]
+        t0, _i, a0 = min(cand, key=lambda c: (c[0], -tail[c[1]]))
+        t, i, a = max((c for c in cand if c[2][0] == a0[0] and c[0] <= t0 + LOOK),
+                      key=lambda c: (tail[c[1]] + PRI.get(ops[c[1]]["grp"] + c[2][0], 0.0), -c[1]))
+        o = ops[i]
+        q = a[0]
+        free[q] = t + a[3]
+        done[i] = t + a[3]
+        if o["lat"]:
+            lat = o["lat"]
+            if o["remote"]:
+                lat += first[0]
+                first[0] = 0.0
+            dma[0] = max(dma[0], t + lat) + o["bytes"] / BW
+            done[i] = dma[0]
+        who[i] = q
+        for b in o["banks"]:
+            bank.setdefault(b, {})[q] = done[i]
+        order.append((i, a))
+        ready.remove(i)
+        for j in succ[i]:
+            left[j] -= 1
+            if not left[j]:
+                ready.append(j)
+    return order, pred, max(done)
+
+
+def rank_program(g, core, T, topo):
+    me = T.rank_of(core)
+    if me is None:
+        return
+    V, S, P = g.vector, g.scalar, g.tensor
+    queue = {"V": V, "S": S, "P": P, "G": g, "Y": g.sync}
+    ops = []
+    stage = ["0", "0"]
+
+    def add(alt, r=(), w=(), banks=(), sem=None, inc=1, lat=0.0, nbytes=0, remote=None, bump=0.0):
+        ops.append(dict(alt=alt, r=list(r), w=list(w), banks=list(banks), sem=sem, inc=inc, lat=lat, bytes=nbytes, remote=remote, bump=bump,
+                        grp=stage[0] + stage[1] + ("2" if len(alt) > 1 else "1")))
+
+    def vec(fn, args, n, r=(), w=(), banks=()):
+        add([("V", fn, (args, {}), max(n, 64) * CYC)], r, w, banks)
+
+    def act(out, in_, n, r=(), w=(), banks=(), **kw):
+        add([("S", S.activation, ((out, in_, IDENT if "bias" in kw else COPY), kw), max(n, 64) * CYC)], r, w, banks)
+
+    def copy(out, in_, n, r=(), w=(), banks=()):
+        add([("S", S.activation, ((out, in_, COPY), {}), max(n, 64) * CYC), ("V", V.tensor_copy, ((out, in_), {}), max(n, 64) * CYC)], r, w, banks)
+
+    def mm(out, lh, rh, start, stop, n, f32, r, w, b):
+        add([("P", P.matmul, ((out, lh, rh, start, stop), {}), max(n, 64) * (4 if f32 else 1) * PEC)], r, list(w) + [("pe", b)], [b])
+
+    def pool(fn, args, n, r=(), w=(), **kw):
+        add([("G", fn, (args, kw), 0.17 + 2 * n * CYC)], r, w)
+
+    def dma(q, out, in_, nbytes, sem, r=(), w=(), bump=0.0):
+        add([(q, queue[q].dma_start, ((out, in_), {}), 0.1)], r, w, sem=sem, inc=16, lat=DMAL, nbytes=nbytes, bump=bump)
+
+    def gcost(q, n):
+        return (0.06 if q == "V" else 0.08) + n * GAT * CYC
+
+    peers = [c for c in T.cores if c != core]
+    mask = topo.mask(core, peers[0])
+    for c in peers:
+        mask &= topo.mask(core, c)
+    neng = bin(mask).count("1")
+    dsts = [DstId(rid=topo.addr(c)[0], pnc=topo.addr(c)[1]) for c in peers]
+    own = NV * me
+
+    def send(win, cols, name, key, size):
+        ap = T[win][:, own:own + cols]
+        tr = RemoteDMATransfer(dst_ids=dsts, dma_engine_mask=mask, remote_sem=T.sem["a" + name], srcs=[ap], dsts=[ap] * len(peers))
+        add([("G", g.remote_dma_fused, (([tr],), {"local_sem": T.sem["l" + name]}), 0.3)], [key], [("halo", name)], sem="l" + name,
+            inc=neng, lat=REML, nbytes=128 * cols * size * len(peers), remote="a" + name)
+
+    def geo(k):
+        cb, n = CH[k]
+        stage[1] = str(k)
+        return n, 128 * cb, 128 * n, 8 * cb, 8 * n, 48 * cb, 48 * n, 768 * cb
+
+    KS = range(len(CH))
+    TT, TS, CP, SCAN, MS = V.tensor_tensor, V.tensor_scalar, V.tensor_copy, V.tensor_tensor_scan, V.memset
+
+    def quarters(c0, cw):
+        return [("Q", j) for j in range(c0 // 256, (c0 + cw + 255) // 256)], [("Pn", j) for j in range(c0 // 256, (c0 + cw + 255) // 256)]
+
+    for j in range(4):
+        dma("Y", T.QW[:, own + 256 * j:own + 256 * j + 256], T.qu[:, 256 * j:256 * j + 256], 131072, "dq%d" % j, w=[("Q", j)], bump=4.0 - j)
+        dma("S", T.Pn[:, 256 * j:256 * j + 256], T.po[:, 256 * j:256 * j + 256], 65536, "dp%d" % j, w=[("Pn", j)], bump=4.0 - j)
+    dma("Y", T.nb3[:], T.nb[:], 196608, "dnb", w=["nb"])
+
+    F = dict(allow_small_or_imprecise_dtypes=True)
+    cf = T.cf
+    jj, ii, pm, pg = cf[:, 0:1], cf[:, 1:2], cf[:, 2:3], cf[:, 3:4]
+    sp, ns, we, idr, cw_, cb_, cc_ = (cf[:, i:i + 1] for i in range(4, 11))
+    pool(g.iota, (T.ci[:, 0:1], [[0, 1]], 0, 1), 1, w=["ci0"])
+    pool(g.iota, (T.gi[:], [[0, 2], [1, 8]], 0, 0), 16, w=["gi"], **F)
+    vec(MS, (T.ones[:], 1.0), 64, w=["ones"])
+    pool(g.affine_select, (T.idn[:], T.ones[:], [[-1, 128]], A.is_equal, 0.0, 0, 1), 128, r=["ones"], w=["idn"])
+    vec(TS, (T.ci[:, 1:2], T.ci[:, 0:1], 3, None, A.bitwise_and), 1, ["ci0"], ["ci1"])
+    vec(TS, (T.ci[:, 2:3], T.ci[:, 0:1], 2, 3, A.arith_shift_right, A.bitwise_and), 1, ["ci0"], ["ci2"])
+    vec(TS, (T.ci[:, 3:4], T.ci[:, 0:1], 15, None, A.bitwise_and), 1, ["ci0"], ["ci3"])
+    vec(TS, (T.ci[:, 4:5], T.ci[:, 0:1], 4, None, A.arith_shift_right), 1, ["ci0"], ["ci4"])
+    vec(CP, (cf[:, 0:4], T.ci[:, 1:5]), 4, ["ci1", "ci2", "ci3", "ci4"], ["cf"])
+    vec(TS, (sp, ii, jj, None, A.is_gt), 1, ["cf"], ["sp"])
+    vec(TS, (ns, ii, jj, None, A.is_le), 1, ["cf"], ["ns"])
+    vec(TS, (we, ii, jj, ns, A.is_lt, A.add), 1, ["cf", "ns"], ["we"])
+    vec(TS, (T.RE[:], T.gi[:, 0:8], pg, we, A.is_equal, A.mult), 8, ["gi", "cf", "we"], ["RE"])
+    vec(TS, (T.dbl[:], T.idn[:], we, None, A.mult), 64, ["idn", "we"], ["dbl"])
+    vec(TS, (idr, pm, 12.0, sp, A.is_ge, A.mult), 1, ["cf", "sp"], ["idr"])
+    vec(TS, (cb_, pm, 3.0, None, A.is_lt), 1, ["cf"], ["cb"])
+    vec(TS, (cc_, pm, 14.0, None, A.is_ge), 1, ["cf"], ["cc"])
+    vec(TS, (cw_, idr, -1.0, 1.0, A.mult, A.add), 1, ["idr"], ["cw"])
+    vec(TS, (T.RA[:, 8:16], T.gi[:, 0:8], pg, idr, A.is_equal, A.mult), 8, ["gi", "cf", "idr"], ["RA1"])
+    vec(MS, (T.sel[:], 0.0), 72, w=["sel"])
+    vec(TS, (T.RB[:], T.gi[:], pg, cb_, A.is_equal, A.mult), 16, ["gi", "cf", "cb"], ["RB"])
+    vec(TS, (T.RA[:, 0:8], T.gi[:, 0:8], pg, cw_, A.is_equal, A.mult), 8, ["gi", "cf", "cw"], ["RA0"])
+    vec(TS, (T.sel[:, 15:143:16], T.gi[:, 0:8], pg, cc_, A.is_equal, A.mult), 8, ["gi", "cf", "cc"], ["sel"])
+    vec(MS, (T.patR[:], 0.0), NEMAX, w=["patR"])
+    vec(MS, (T.patK[:], 1.0), NEMAX, w=["patK"])
+    vec(MS, (T.tz[:], 0.0), 384, w=[("tz", k) for k in KS])
+    vec(MS, (T.patR[:, 0:NEMAX:6], RESET), 1, w=["patR"])
+    vec(MS, (T.patK[:, 0:NEMAX:6], 0.0), 1, w=["patK"])
+    vec(MS, (T.QW[:, ZERO:ZERO + 8], 0.0), 1, w=["qz"])
+    vec(MS, (T.dl[:, 0:384:48], 0.0), 1, w=[("dl", k) for k in KS])
+    act(T.bigi[:], T.idn[:], 128, ["idn"], ["bigi"], scale=BIG)
+    act(T.idf[:], T.idn[:], 128, ["idn"], ["idf"])
+    RC = T.sel[:, 15:143:16]
+    for k in KS:
+        n, c0, cw, vo, w, eo, ne, go = geo(k)
+        X = T["X1%d" % k]
+        vec(MS, (X[:], 0.0), 64 * n, w=[("X1", k)])
+        pool(g.iota, (X[:, :, 12 * n:13 * n], [[0, 8], [128, n]], own + c0, 0), w, w=[("X1", k)], **F)
+        pool(g.iota, (X[:, :, 13 * n:14 * n], [[0, 8], [0, n]], 0, 1), w, w=[("X1", k)], **F)
+        pool(g.iota, (T.vT[:, eo:eo + ne], [[0, 8], [128, n], [0, 6]], own + c0, 1), ne, w=[("vT", k)], **F)
+        pool(g.iota, (T["X2%d" % k][:], [[0, 8], [0, 16 * n]], 0, 0), 128 * n, w=[("X2", k)], **F)
+        pool(g.iota, (T.vL[:, eo:eo + ne], [[0, 6], [16, w]], own + c0, 0), ne, w=["vL"], **F)
+        vec(TS, (T.off1[:, eo:eo + ne], T.nb3[:, :, vo:vo + w], float(-own if k else 0), None, A.add), ne, ["nb"], [("off1", k)])
+        vec(TS, (T.nbz[:, eo:eo + ne], T.nb3[:, :, vo:vo + w], float(-ZERO), None, A.add), ne, ["nb"], [("nbz", k)])
+    act(T.vL[:], T.vL[:], 384, ["cf", "vL"], ["vL"], bias=pm)
+
+    def digits3(k, src, rk, banks, X, xk, rows):
+        n, c0, cw, vo, w, eo, ne, go = geo(k)
+        h, m, lo = (X[:, :, r * n:(r + 1) * n] for r in rows)
+        rem = T.tm[:, vo:vo + w]
+        vec(CP, (h, src), w, rk, [xk], banks)
+        vec(TT, (rem, src, h, A.subtract), 2 * w, rk + [xk], [("tm", k)], banks)
+        vec(CP, (m, rem), w, [("tm", k)], [xk])
+        vec(TT, (lo, rem, m, A.subtract), 2 * w, [("tm", k), xk], [xk])
+
+    wturn = [0]
+
+    def window(k, win, kind):
+        n, c0, cw, vo, w, eo, ne, go = geo(k)
+        b = "wa%d" % (wturn[0] % 2)
+        wturn[0] += 1
+        ps, X1, X2 = T[b], T["X1%d" % k], T["X2%d" % k]
+        if kind == "P":
+            mm(ps[:, 0:cw], T.dbl[:], T.Pn[:, c0:c0 + cw], True, False, cw, False, ["dbl"] + quarters(c0, cw)[1], [b], b)
+            for j in range(n):
+                mm(ps[:, 128 * j:128 * j + 128], X1[:, :, j:16 * n:n], T.idn[:], False, j == n - 1, 128, False, [("X1", k), "idn"], [b], b)
+        else:
+            for j in range(n):
+                o = ps[:, 128 * j:128 * j + 128]
+                mm(o, X2[:, :, j:16 * n:n], T.idn[:], True, kind != "sum", 128, False, [("X2", k), "idn"], [b], b)
+                if kind == "sum":
+                    mm(o, X1[:, :, j:16 * n:n], T.idn[:], False, True, 128, False, [("X1", k), "idn"], [b], b)
+        copy(T[win][:, own + c0:own + c0 + cw], ps[:, 0:cw], cw, [b], [(win, k)], [b])
+
+    def view(win, halo, k):
+        keys = [(win, j) for j in KS]
+        if k == 0:
+            return T[win][:, 0:8192], keys + [("halo", halo)]
+        return T[win][:, own:own + NV], keys
+
+    def gather(qs, dst, src, n, r, w):
+        alt = {"V": ("V", CP, ((dst, src), {}), gcost("V", n)), "S": ("S", S.activation, ((dst, src, COPY), {}), gcost("S", n))}
+        add([alt[q] for q in qs], r, w)
+
+    def to_dense(k, buf, blocks, rhs, rk, width, first, last, f32):
+        n, c0, cw, vo, w, eo, ne, go = geo(k)
+        b_ = "tk%d" % k
+        for i, b in enumerate(blocks):
+            s, j = divmod(b, n)
+            mm(T[b_][:, 6 * j + s:width:6 * n], T[buf][:, go + 128 * b:go + 128 * b + 128], rhs, first,
+               first or (last and i == len(blocks) - 1), 16, f32, [(buf, k, b)] + rk, [("tk", k)], b_)
+
+    def cost(k, name, win, off, gbuf, rhs, rk, width, first):
+        n, c0, cw, vo, w, eo, ne, go = geo(k)
+        wv, wk = view(win, win, k)
+        for s in range(6):
+            dst = T.PR[:, go + cw * s:go + cw * s + cw]
+            ks = [("PR", k, b) for b in range(s * n, s * n + n)]
+            src = wv.indirect(T[off][:, eo + w * s:eo + w * s + w])
+            if s < VS[name][k]:
+                add([("V", TT, ((dst, src, T.Qs[:, c0:c0 + cw], A.mult), {}), gcost("V", cw))], wk + [(off, k), ("Qs", k)], ks)
+            else:
+                gb = T[gbuf][:, go + cw * s:go + cw * s + cw]
+                gk = [(gbuf, k, b) for b in range(s * n, s * n + n)]
+                gather("S", gb, src, cw, wk + [(off, k)], gk)
+                vec(TT, (dst, gb, T["qk%d" % k][:, 0:cw], A.mult), cw, gk + [("qk", k)], ks, ["qk%d" % k])
+            to_dense(k, "PR", range(s * n, s * n + n), rhs, rk, width, first, s == 5, True)
+
+    def best(k):
+        n, c0, cw, vo, w, eo, ne, go = geo(k)
+        vec(SCAN, (T.Mn[:, eo:eo + ne], T.patR[:, 0:ne], T["tk%d" % k][:, 0:ne], 0.0, A.add, A.min), ne,
+            ["patR", ("tk", k)], [("Mn", k)], ["tk%d" % k])
+        digits3(k, T.Mn[:, eo + 5:eo + ne:6], [("Mn", k)], [], T["X2%d" % k], ("X2", k), (0, 1, 2))
+
+    def steps(k, at):
+        n, c0, cw, vo, w, eo, ne, go = geo(k)
+        tk = T["tk%d" % k]
+        copy(T.ids[:, eo:eo + ne], tk[:, at:at + ne], ne, [("tk", k)], [("ids", k)], ["tk%d" % k])
+        vec(TT, (T.dl[:, eo + 1:eo + ne], T.ids[:, eo:eo + ne - 1], tk[:, at + 1:at + ne], A.subtract), ne,
+            [("tk", k), ("ids", k)], [("dl", k)], ["tk%d" % k])
+        vec(TT, (T.to[:, vo:vo + w], T.vT[:, eo:eo + ne:6], tk[:, at + 5:at + ne:6], A.subtract), w,
+            [("tk", k), ("vT", k)], [("to", k)], ["tk%d" % k])
+
+    def choice(k):
+        n, c0, cw, vo, w, eo, ne, go = geo(k)
+        tk = T["tk%d" % k]
+        vec(TT, (T.kp[:, eo + 1:eo + ne], tk[:, 1:ne], T.Mn[:, eo:eo + ne - 1], A.is_ge), ne, [("tk", k), ("Mn", k)], [("kp", k)], ["tk%d" % k])
+        add([("S", S.activation, ((T.kp[:, eo:eo + ne:6], T.vT[:, eo:eo + ne:6], COPY), {"scale": 0.0}), 64 * CYC),
+             ("V", MS, ((T.kp[:, eo:eo + ne:6], 0.0), {}), 64 * CYC)], [("vT", k)], [("kp", k)])
+        vec(SCAN, (T.sd[:, eo:eo + ne], T.dl[:, eo:eo + ne], T.kp[:, eo:eo + ne], 0.0, A.add, A.mult), ne, [("dl", k), ("kp", k)], [("sd", k)])
+        vec(TT, (T.dch[:, vo:vo + w], T.sd[:, eo + 5:eo + ne:6], T.to[:, vo:vo + w], A.subtract), 2 * w, [("sd", k), ("to", k)], [("dch", k)])
+
+    def collapse(k, rows, xl):
+        n, c0, cw, vo, w, eo, ne, go = geo(k)
+        tn, tm = T.tn[:, vo:vo + w], T.tm[:, vo:vo + w]
+        h, lo = T["X2%d" % k][:, :, rows[0] * n:(rows[0] + 1) * n], T[xl + str(k)][:, :, rows[1] * n:(rows[1] + 1) * n]
+        vec(SCAN, (T.sc[:, eo:eo + ne], T.patR[:, 0:ne], T["tk%d" % k][:, 0:ne], 0.0, A.add, A.min), ne,
+            ["patR", ("tk", k)], [("sc", k)], ["tk%d" % k])
+        vec(TT, (tn, T.sc[:, eo + 5:eo + ne:6], T.Mn[:, eo + 5:eo + ne:6], A.is_gt), 2 * w, [("sc", k), ("Mn", k)], [("tn", k)])
+        vec(TT, (tm, tn, T.dch[:, vo:vo + w], A.mult), 2 * w, [("tn", k), ("dch", k)], [("tm", k)])
+        vec(TT, (tn, tm, T.vT[:, eo:eo + ne:6], A.add), 2 * w, [("tm", k), ("vT", k)], [("tn", k)])
+        vec(CP, (h, tn), w, [("tn", k)], [("X2", k)])
+        vec(TT, (lo, tn, h, A.subtract), 2 * w, [("tn", k), ("X2", k)], [(xl, k)])
+
+    def pure(k, win, halo, off, gbuf):
+        n, c0, cw, vo, w, eo, ne, go = geo(k)
+        wv, wk = view(win, halo, k)
+        for b0 in range(0, 6 * n, PIECE):
+            b1 = min(b0 + PIECE, 6 * n)
+            gather("SV", T[gbuf][:, go + 128 * b0:go + 128 * b1], wv.indirect(T[off][:, eo + 8 * b0:eo + 8 * b1]), 128 * (b1 - b0),
+                   wk + [(off, k)], [(gbuf, k, b) for b in range(b0, b1)])
+
+    stage[0] = "W"
+    for k in KS:
+        n, c0, cw, vo, w, eo, ne, go = geo(k)
+        tk, qk = T["tk%d" % k], T["qk%d" % k]
+        for h0 in range(0, cw, 256):
+            h1 = min(h0 + 256, cw)
+            qk_, pk_ = quarters(c0 + h0, h1 - h0)
+            act(qk[:, h0:h1], T.QW[:, own + c0 + h0:own + c0 + h1], h1 - h0, qk_ + ["sp", "ns"], [("qk", k)], ["qk%d" % k], bias=sp, scale=ns)
+            vec(TT, (T.PR[:, go + h0:go + h1], T.Pn[:, c0 + h0:c0 + h1], qk[:, h0:h1], A.mult), h1 - h0, pk_ + [("qk", k)],
+                [("PR", k, b) for b in range(h0 // 128, h1 // 128)], ["qk%d" % k])
+        for j in range(n):
+            mm(tk[:, j:w:n], T.PR[:, go + 128 * j:go + 128 * j + 128], T.RE[:], True, True, 8, True, [("PR", k, j), "RE"], [("tk", k)], "tk%d" % k)
+        digits3(k, tk[:, 0:w], [("tk", k)], ["tk%d" % k], T["X1%d" % k], ("X1", k), (4, 8, 9))
+        copy(T.Es[:, vo:vo + w], tk[:, 0:w], w, [("tk", k)], [("Es", k)], ["tk%d" % k])
+        window(k, "W1", "P")
+        act(T.Qs[:, c0:c0 + cw], T.QW[:, own + c0:own + c0 + cw], cw, quarters(c0, cw)[0] + ["sp", "ns"], [("Qs", k)], bias=sp, scale=ns)
+    for j in range(4):
+        act(T.QW[:, own + 256 * j:own + 256 * j + 256], T.QW[:, own + 256 * j:own + 256 * j + 256], 256, [("Q", j), "ns"], [("Q", j)], scale=ns)
+    send("W1", 128, "W1", ("W1", 0), 2)
+    send("QW", 128, "Q", ("Q", 0), 4)
+    for s in range(6):
+        act(T.Er[:, s:384:6], T.Es[:], 64, [("Es", k) for k in KS], [("Er", s)], scale=-1.0)
+
+    stage[0] = "A"
+    for k in KS:
+        n, c0, cw, vo, w, eo, ne, go = geo(k)
+        cost(k, "A", "W1", "off1", "GA", T.RA[:], ["RA0", "RA1"], 2 * ne, True)
+        best(k)
+        window(k, "WB", "X")
+        vec(TT, (T.tz[:, 2 * eo:2 * eo + ne], T.vT[:, eo:eo + ne], T["tk%d" % k][:, ne:2 * ne], A.is_lt), ne,
+            [("vT", k), ("tk", k)], [("tz", k)], ["tk%d" % k])
+        steps(k, ne)
+        choice(k)
+    send("WB", 128, "WB", ("WB", 0), 2)
+
+    stage[0] = "B"
+    for k in KS:
+        n, c0, cw, vo, w, eo, ne, go = geo(k)
+        b_ = "tk%d" % k
+        pure(k, "WB", "WB", "off1", "GB")
+        mm(T[b_][:, 0:2 * ne], T.idn[:], T.tz[:, 2 * eo:2 * eo + 2 * ne], True, False, 2 * ne, False, ["idn", ("tz", k)], [("tk", k)], b_)
+        mm(T[b_][:, ne:2 * ne], T.idf[:], T.Er[:, eo:eo + ne], False, False, ne, True, ["idf"] + [("Er", s) for s in range(6)], [("tk", k)], b_)
+        to_dense(k, "GB", range(6 * n), T.RB[:], ["RB"], 2 * ne, False, True, False)
+        collapse(k, (14, 15), "X2")
+        window(k, "WC", "X")
+    send("WC", 128, "WC", ("WC", 0), 2)
+
+    stage[0] = "C"
+    for k in KS:
+        n, c0, cw, vo, w, eo, ne, go = geo(k)
+        b_ = lb = "tk%d" % k
+        tk = T[b_]
+        L = tk[:, 2 * ne:3 * ne]
+        pure(k, "WC", "WC", "off1", "GA")
+        to_dense(k, "GA", range(6 * n), RC, ["sel"], ne, True, True, False)
+        for r in range(16):
+            mm(L, T.sel[:, 15 - r:143 - r], T.GA[:, go + r:go + 6 * cw:16], r == 0, r == 15, ne, False,
+               [("GA", k, b) for b in range(6 * n)] + ["sel"], [("L", k)], lb)
+        vec(TS, (T.offE[:, eo:eo + ne], L, float(-own if k else 0), None, A.add), ne, [("L", k)], [("offE", k)], [lb])
+        vec(TT, (L, L, T.vL[:, eo:eo + ne], A.is_equal), ne, [("L", k), "vL"], [("L", k)], [lb])
+        vec(TT, (T.xL[:, eo:eo + ne], L, T.nbz[:, eo:eo + ne], A.mult), ne, [("L", k), ("nbz", k)], [("xL", k)], [lb])
+        vec(TS, (T.offD[:, eo:eo + ne], T.xL[:, eo:eo + ne], float(ZERO), None, A.add), ne, [("xL", k)], [("offD", k)])
+        vec(TT, (T.ab[:, eo:eo + ne], tk[:, 0:ne], T.vT[:, eo:eo + ne], A.is_equal), ne, [("tk", k), ("vT", k)], [("ab", k)], [b_])
+        vec(TT, (T.kp[:, eo:eo + ne], T.ab[:, eo:eo + ne], tk[:, ne:2 * ne], A.mult), ne, [("ab", k), ("tk", k)], [("kp", k)], [b_])
+        vec(SCAN, (T.sc[:, eo:eo + ne], T.patK[:, 0:ne], T.kp[:, eo:eo + ne], 0.0, A.mult, A.add), ne, ["patK", ("kp", k)], [("sc", k)])
+        vec(TT, (T.tn[:, vo:vo + w], T.sc[:, eo + 5:eo + ne:6], T.Es[:, vo:vo + w], A.add), 2 * w, [("sc", k), ("Es", k)], [("tn", k)])
+        digits3(k, T.tn[:, vo:vo + w], [("tn", k)], [], T["X1%d" % k], ("X1", k), (4, 8, 9))
+        window(k, "W2", "P")
+        vec(TT, (T.t2[:, eo:eo + ne], T.vT[:, eo:eo + ne], tk[:, 0:ne], A.is_lt), ne, [("vT", k), ("tk", k)], [("t2", k)], [b_])
+        steps(k, 0)
+    send("W2", 256, "W2", ("W2", 0), 2)
+
+    stage[0] = "D"
+    QK = [("Q", j) for j in range(4)] + [("halo", "Q"), "qz"]
+    at = 0
+    for k in KS:
+        n, c0, cw, vo, w, eo, ne, go = geo(k)
+        b_ = "qk%d" % k
+        for s in range(6):
+            src = T.QW[:, 0:8200].indirect(T.offD[:, eo + w * s:eo + w * s + w])
+            if s < VS["D"][k]:
+                add([("V", TT, ((T.acc[:, c0:c0 + cw], src, (T.acc if s else T.Qs)[:, c0:c0 + cw], A.add), {}), gcost("V", cw))],
+                    QK + [("offD", k), ("acc", k), ("Qs", k)], [("acc", k)])
+            else:
+                gather("S", T.GD[:, at:at + cw], src, cw, QK + [("offD", k)], [("GD", k, s)])
+                mm(T[b_][:, 0:cw], T.idf[:], T.GD[:, at:at + cw], s == VS["D"][k], s == 5, cw, True, [("GD", k, s), "idf"], [("qk", k)], b_)
+                at += cw
+        vec(TT, (T.Qs[:, c0:c0 + cw], T.acc[:, c0:c0 + cw], T[b_][:, 0:cw], A.add), cw, [("acc", k), ("qk", k)], [("Qs", k)], [b_])
+        copy(T[b_][:, 0:cw], T.Qs[:, c0:c0 + cw], cw, [("Qs", k)], [("qk", k)], [b_])
+        dma("Y", T.q1[:, c0:c0 + cw], T.Qs[:, c0:c0 + cw], 512 * cw, "do%d" % k, [("Qs", k)], [("q1", k)])
+    QS = [("Qs", k) for k in KS]
+
+    stage[0] = "E"
+    for k in KS:
+        n, c0, cw, vo, w, eo, ne, go = geo(k)
+        b_ = "tk%d" % k
+        mm(T[b_][:, 0:ne], T.bigi[:], T.ab[:, eo:eo + ne], True, False, ne, False, ["bigi", ("ab", k)], [("tk", k)], b_)
+        cost(k, "E", "W2", "offE", "GB", T.RA[:, 0:8], ["RA0"], ne, False)
+        if k == 0:
+            for r in range(16):
+                mm(T.wa1[:, 0:64], T.sel[:, 15 - r:143 - r], T.WC[:, own + r:own + NV:16], r == 0, r == 15, 64, False,
+                   [("WC", j) for j in KS] + ["sel"], ["wa1"], "wa1")
+            vec(CP, (T.offG[:, 0:8], T.wa1[:, 0:8]), 8, ["wa1"], ["offG0"], ["wa1"])
+            vec(TS, (T.offG[:, 8:64], T.wa1[:, 8:64], float(-own), None, A.add), 56, ["wa1"], ["offG1"], ["wa1"])
+            wturn[0] = 0
+        best(k)
+        window(k, "WB", "X")
+        choice(k)
+    send("WB", 256, "WF", ("WB", 0), 2)
+    for i, (a, b) in enumerate((a, b) for a in range(4) for b in range(a)):
+        dma("Y", T.q1[4 * a + b:128:16, :], T.Qs[4 * b + a:128:16, :], 32768, "df%d" % i,
+            QS + [("q1", k) for k in KS] + [("halo", "WF")], [("q1f", i)])
+
+    stage[0] = "F"
+    for k in KS:
+        n, c0, cw, vo, w, eo, ne, go = geo(k)
+        b_ = "tk%d" % k
+        pure(k, "WB", "WF", "offE", "GA")
+        mm(T[b_][:, 0:ne], T.idn[:], T.t2[:, eo:eo + ne], True, False, ne, False, ["idn", ("t2", k)], [("tk", k)], b_)
+        mm(T[b_][:, 0:ne], T.bigi[:], T.ab[:, eo:eo + ne], False, False, ne, False, ["bigi", ("ab", k)], [("tk", k)], b_)
+        to_dense(k, "GA", range(6 * n), T.RB[:, 0:8], ["RB"], ne, False, True, False)
+        collapse(k, (0, 0), "X1")
+        window(k, "WG", "sum")
+    send("WG", 128, "WG", ("WG", 0), 4)
+
+    stage[0] = "G"
+    GK = [("WG", k) for k in KS] + QS
+    gather("V", T.acc[:, 128:576], T.WG[:, own:own + NV].indirect(T.offG[:, 8:36]), 448, GK + ["offG1"], ["g1"])
+    gather("S", T.acc[:, 576:1024], T.WG[:, own:own + NV].indirect(T.offG[:, 36:64]), 448, GK + ["offG1"], ["g2"])
+    gather("VS", T.acc[:, 0:128], T.WG[:, 0:8192].indirect(T.offG[:, 0:8]), 128, GK + [("halo", "WG"), "offG0"], ["g0"])
+    dma("Y", T.goal[:], T.acc[0:128:16, :], 32768, "dgo", ["g0", "g1", "g2"])
+
+    order, pred, _t = arrange(ops)
+    count, waited, mark, bank = {}, {}, {}, {}
+
+    def wait(q, sem, val):
+        if waited.get((q, sem), 0) < val:
+            queue[q].wait_ge(T.sem[sem], val)
+            waited[(q, sem)] = val
+
+    for i, (q, fn, (args, kw), _c) in order:
+        o = ops[i]
+        need = {}
+        marks = [t for j in pred[i] for t in mark[j]] + [t for b in o["banks"] for q2, t in bank.get(b, {}).items() if q2 != q]
+        for sem, val in marks:
+            if not (q == "P" and sem == "cP"):
+                need[sem] = max(need.get(sem, 0), val)
+        for sem, val in need.items():
+            wait(q, sem, val)
+        ins = fn(*args, **kw)
+        sem = o["sem"] or "c" + q
+        count[sem] = count.get(sem, 0) + o["inc"]
+        mark[i] = [(sem, count[sem])]
+        if o["remote"]:
+            count[o["remote"]] = neng * len(peers)
+            mark[i].append((o["remote"], count[o["remote"]]))
+        else:
+            ins.then_inc(T.sem[sem], o["inc"])
+        for b in o["banks"]:
+            bank.setdefault(b, {})[q] = mark[i][0]
+    for sem, val in count.items():
+        wait("Y" if sem in ("dgo", "cV", "cS") else "G", sem, val)

@@ -10,18 +10,18 @@ BIG = float(1 << 26)
 RESET = float(1 << 29)
 ZERO = 8192
 VS = {"A": (2, 2, 2), "D": (4, 3, 3), "E": (1, 1, 2)}
-PIECE = 6
+PIECE = 4
 NEMAX = 48 * max(n for _c, n in CH)
-CYC, GAT, PEC, WAKE, DMAL, REML, FIRST, BW, LOOK, SHARE = 0.00104, 1.5, 0.00055, 0.08, 2.0, 3.6, 2.0, 200000.0, 0.12, 0.3
-PRI = {'W02V': -14.5, 'F02S': 1.0, 'A02V': 6.5, 'D02V': 3.5, 'E12V': -0.5, 'B01V': 9.5, 'A12V': -17.5, 'E12S': 42.0, 'W01V': 11.0,
-       'G21V': -2.0, 'W22V': 4.5, 'A22S': -6.0, 'E01V': -2.0, 'F12V': -12.0, '021V': 1.0, 'A11S': -5.5, 'B22V': 2.5, 'E22V': -1.5,
-       'W22S': -7.0, 'W12V': -3.0, 'W21V': 2.5, 'D22S': 13.0, 'W11V': -1.0, 'F11V': -4.0, '011V': 5.0, 'D22V': -8.5, 'E01S': -3.5,
-       '021S': -11.5, 'D12S': 29.0, 'A21S': 5.5, 'D12V': -20.0, 'C02V': 20.0, 'D01S': -5.5, 'F01V': 8.5, 'A01S': 0.5, 'E21S': -19.5,
-       'F02V': 7.0, 'W12S': -4.5, 'A22V': -9.0, 'C12S': -5.5, '001S': -8.5, 'A01V': 1.5, 'C12V': -22.0, 'A02S': 18.0, 'F21V': 10.0,
-       'C02S': 6.0, 'G22V': 20.5, 'W01S': -23.5, 'D21S': -4, 'W02S': 19.5, 'A12S': -2.0, 'G22S': 14.5, 'B02V': 35.5, 'F12S': -3.0,
-       'C22S': 0.5, 'E22S': 9.0, 'B12V': 6.5, 'E02V': -10.0, 'F22V': 1.5, 'W11S': -11.0, 'C01V': 28.5, 'E02S': 25.5, 'B12S': 2.0,
-       'D02S': 8.5, 'G21S': 4.0, 'B22S': -13.0, '001V': 2.0, 'F22S': 1.5, 'D11S': 1.0, 'W21S': -20.0, 'B02S': 12.5, 'E11S': -0.5,
-       'C22V': 5.0, 'D21V': -1}
+CYC, GAT, PEC, WAKE, DMAL, REML, FIRST, BW, LOOK, SHARE = 0.001, 1.56, 0.00055, 0.17, 2.0, 3.2, 2.0, 200000.0, 0.05, 0.3
+PRI = {'D22S': -14.0, '021S': -7.5, 'W22V': 30.0, 'A21V': 1.5, 'B21V': -10.0, 'B11V': -0.5, 'W12V': 37.0, 'B12S': -14.0, 'B22V': 0.5,
+       '011V': 11.0, 'E12S': -20.0, 'D02V': -13.5, 'W02V': 38.0, 'A02V': -13.5, 'D22V': 5.0, 'W02S': -5.5, 'E22S': 15.0, 'C12V': -9.0,
+       'F21V': -26.5, 'F22V': -10.5, 'C01V': -1.0, 'B02S': 15.5, 'D01S': 7.0, 'D11S': -4.0, '021V': -1.5, 'W11S': -44.0, 'C21V': 2.5,
+       'A22V': 41.5, 'W21S': 27.5, 'E22V': 27.0, 'F22S': -44.0, 'F02S': 3.0, 'F11V': -8.0, 'D02S': 4.5, 'D12S': 16.5, 'F01V': 3.5,
+       'G22S': 7.0, 'W12S': -53.0, 'C12S': 3.5, 'A12V': -30.0, 'G21V': -6.0, 'W01S': -3.0, 'W11V': 7.5, 'E02S': -6.5, 'C22S': -3.0,
+       '001V': 9.5, 'W22S': 18.5, 'F02V': 30.5, 'D12V': -55.0, 'B02V': 37.5, 'A22S': -7.5, 'G22V': -12.0, 'A12S': 18.0, 'A02S': 38.0,
+       'W01V': -0.5, 'C02S': 2.5, 'B01V': 64.5, 'A01S': 10.5, 'A11S': 11.5, 'E01S': 1.0, 'B12V': 18.0, 'W21V': -0.5, 'G21S': -21.5,
+       'F12S': -2.0, 'A01V': 3.5, 'C22V': -38.0, 'E21S': -22.0, 'A21S': -13.0, '001S': -7.5, 'F12V': -3.5, 'E02V': -8.5, 'D21S': 23.5,
+       'E11V': 1.0, 'E12V': 11.0, 'A11V': 5.5, 'C11V': 4.0, 'C02V': -8.5, 'D01V': -1, 'B22S': -17.0, 'E11S': 2.0, 'E21V': -4.0}
 
 SCRATCH = {"nb3": ("sbuf", [128, 6, 64], "int32"), "ci": ("sbuf", [128, 8], "int32")}
 for _names, _cols, _dt in [
@@ -228,9 +228,10 @@ def rank_program(g, core, T, topo):
         pool(g.iota, (X[:, :, 13 * n:14 * n], [[0, 8], [0, n]], 0, 1), w, w=[("X1", k)], **F)
         pool(g.iota, (T.vT[:, eo:eo + ne], [[0, 8], [128, n], [0, 6]], own + c0, 1), ne, w=[("vT", k)], **F)
         pool(g.iota, (T["X2%d" % k][:], [[0, 8], [0, 16 * n]], 0, 0), 128 * n, w=[("X2", k)], **F)
-        pool(g.iota, (T.vL[:, eo:eo + ne], [[0, 6], [16, w]], own + c0, 0), ne, w=["vL"], **F)
-        vec(TS, (T.off1[:, eo:eo + ne], T.nb3[:, :, vo:vo + w], float(-own if k else 0), None, A.add), ne, ["nb"], [("off1", k)])
-        vec(TS, (T.nbz[:, eo:eo + ne], T.nb3[:, :, vo:vo + w], float(-ZERO), None, A.add), ne, ["nb"], [("nbz", k)])
+        pool(g.iota, (T.vL[:, eo:eo + ne], [[0, 6], [16, w]] if k else [[128, 2], [0, 6], [16, 8]], own + c0, 0), ne, w=["vL"], **F)
+        for e0, e1, v0, v1 in ([(eo, eo + ne, vo, vo + w)] if k else [(0, 48, 0, 8), (48, 96, 8, 16)]):
+            vec(TS, (T.off1[:, e0:e1], T.nb3[:, :, v0:v1], float(-own if e0 else 0), None, A.add), e1 - e0, ["nb"], [("off1", k)])
+            vec(TS, (T.nbz[:, e0:e1], T.nb3[:, :, v0:v1], float(-ZERO), None, A.add), e1 - e0, ["nb"], [("nbz", k)])
     act(T.vL[:], T.vL[:], 384, ["cf", "vL"], ["vL"], bias=pm)
 
     def digits3(k, src, rk, banks, X, xk, rows):
@@ -261,11 +262,18 @@ def rank_program(g, core, T, topo):
                     mm(o, X1[:, :, j:16 * n:n], T.idn[:], False, True, 128, False, [("X1", k), "idn"], [b], b)
         copy(T[win][:, own + c0:own + c0 + cw], ps[:, 0:cw], cw, [b], [(win, k)], [b])
 
-    def view(win, halo, k):
+    def units(k):
+        n = CH[k][1]
+        return [(s, s * n, n, 0) for s in range(6)] if k else [(s, 6 * j + s, 1, 128 * j) for j in (1, 0) for s in range(6)]
+
+    def view(win, halo, far):
         keys = [(win, j) for j in KS]
-        if k == 0:
+        if far:
             return T[win][:, 0:8192], keys + [("halo", halo)]
         return T[win][:, own:own + NV], keys
+
+    def blocks(k):
+        return [b for s, b0, m, x0 in units(k) for b in range(b0, b0 + m)]
 
     def gather(qs, dst, src, n, r, w):
         alt = {"V": ("V", CP, ((dst, src), {}), gcost("V", n)), "S": ("S", S.activation, ((dst, src, COPY), {}), gcost("S", n))}
@@ -275,25 +283,28 @@ def rank_program(g, core, T, topo):
         n, c0, cw, vo, w, eo, ne, go = geo(k)
         b_ = "tk%d" % k
         for i, b in enumerate(blocks):
-            s, j = divmod(b, n)
+            s, j = divmod(b, n) if k else (b % 6, b // 6)
             mm(T[b_][:, 6 * j + s:width:6 * n], T[buf][:, go + 128 * b:go + 128 * b + 128], rhs, first,
                first or (last and i == len(blocks) - 1), 16, f32, [(buf, k, b)] + rk, [("tk", k)], b_)
 
     def cost(k, name, win, off, gbuf, rhs, rk, width, first):
         n, c0, cw, vo, w, eo, ne, go = geo(k)
-        wv, wk = view(win, win, k)
-        for s in range(6):
-            dst = T.PR[:, go + cw * s:go + cw * s + cw]
-            ks = [("PR", k, b) for b in range(s * n, s * n + n)]
-            src = wv.indirect(T[off][:, eo + w * s:eo + w * s + w])
+        for i, (s, b0, m, x0) in enumerate(units(k)):
+            wv, wk = view(win, win, k == 0 and (x0 == 0 or off != "off1"))
+            g0, g1, xw = go + 128 * b0, go + 128 * (b0 + m), 128 * m
+            ks = [("PR", k, b) for b in range(b0, b0 + m)]
+            src = wv.indirect(T[off][:, eo + 8 * b0:eo + 8 * (b0 + m)])
             if s < VS[name][k]:
-                add([("V", TT, ((dst, src, T.Qs[:, c0:c0 + cw], A.mult), {}), gcost("V", cw))], wk + [(off, k), ("Qs", k)], ks)
+                add([("V", TT, ((T.PR[:, g0:g1], src, T.Qs[:, c0 + x0:c0 + x0 + xw], A.mult), {}), gcost("V", xw))],
+                    wk + [(off, k), ("Qs", k)], ks)
             else:
-                gb = T[gbuf][:, go + cw * s:go + cw * s + cw]
-                gk = [(gbuf, k, b) for b in range(s * n, s * n + n)]
-                gather("S", gb, src, cw, wk + [(off, k)], gk)
-                vec(TT, (dst, gb, T["qk%d" % k][:, 0:cw], A.mult), cw, gk + [("qk", k)], ks, ["qk%d" % k])
-            to_dense(k, "PR", range(s * n, s * n + n), rhs, rk, width, first, s == 5, True)
+                gk = [(gbuf, k, b) for b in range(b0, b0 + m)]
+                if (s - VS[name][k]) % 2 == 0:
+                    b1 = b0 + m * min(2, 6 - s)
+                    gather("S", T[gbuf][:, g0:go + 128 * b1], wv.indirect(T[off][:, eo + 8 * b0:eo + 8 * b1]), 128 * (b1 - b0),
+                           wk + [(off, k)], [(gbuf, k, b) for b in range(b0, b1)])
+                vec(TT, (T.PR[:, g0:g1], T[gbuf][:, g0:g1], T["qk%d" % k][:, x0:x0 + xw], A.mult), xw, gk + [("qk", k)], ks, ["qk%d" % k])
+            to_dense(k, "PR", range(b0, b0 + m), rhs, rk, width, first, i == len(units(k)) - 1, True)
 
     def best(k):
         n, c0, cw, vo, w, eo, ne, go = geo(k)
@@ -333,9 +344,8 @@ def rank_program(g, core, T, topo):
 
     def pure(k, win, halo, off, gbuf):
         n, c0, cw, vo, w, eo, ne, go = geo(k)
-        wv, wk = view(win, halo, k)
-        for b0 in range(0, 6 * n, PIECE):
-            b1 = min(b0 + PIECE, 6 * n)
+        for b0, b1 in ([(b, min(b + PIECE, 6 * n)) for b in range(0, 6 * n, PIECE)] if k else [(6, 9), (9, 12), (0, 3), (3, 6)]):
+            wv, wk = view(win, halo, k == 0 and (b0 < 6 or off != "off1"))
             gather("SV", T[gbuf][:, go + 128 * b0:go + 128 * b1], wv.indirect(T[off][:, eo + 8 * b0:eo + 8 * b1]), 128 * (b1 - b0),
                    wk + [(off, k)], [(gbuf, k, b) for b in range(b0, b1)])
 
@@ -381,7 +391,7 @@ def rank_program(g, core, T, topo):
         pure(k, "WB", "WB", "off1", "GB")
         mm(T[b_][:, 0:2 * ne], T.idn[:], T.tz[:, 2 * eo:2 * eo + 2 * ne], True, False, 2 * ne, False, ["idn", ("tz", k)], [("tk", k)], b_)
         mm(T[b_][:, ne:2 * ne], T.idf[:], T.Er[:, eo:eo + ne], False, False, ne, True, ["idf"] + [("Er", s) for s in range(6)], [("tk", k)], b_)
-        to_dense(k, "GB", range(6 * n), T.RB[:], ["RB"], 2 * ne, False, True, False)
+        to_dense(k, "GB", blocks(k), T.RB[:], ["RB"], 2 * ne, False, True, False)
         collapse(k, (14, 15), "X2")
         window(k, "WC", "X")
     send("WC", 128, "WC", ("WC", 0), 2)
@@ -393,7 +403,7 @@ def rank_program(g, core, T, topo):
         tk = T[b_]
         L = tk[:, 2 * ne:3 * ne]
         pure(k, "WC", "WC", "off1", "GA")
-        to_dense(k, "GA", range(6 * n), RC, ["sel"], ne, True, True, False)
+        to_dense(k, "GA", blocks(k), RC, ["sel"], ne, True, True, False)
         for r in range(16):
             mm(L, T.sel[:, 15 - r:143 - r], T.GA[:, go + r:go + 6 * cw:16], r == 0, r == 15, ne, False,
                [("GA", k, b) for b in range(6 * n)] + ["sel"], [("L", k)], lb)
@@ -417,16 +427,21 @@ def rank_program(g, core, T, topo):
     for k in KS:
         n, c0, cw, vo, w, eo, ne, go = geo(k)
         b_ = "qk%d" % k
-        for s in range(6):
-            src = T.QW[:, 0:8200].indirect(T.offD[:, eo + w * s:eo + w * s + w])
+        for s, b0, m, x0 in units(k):
+            src = T.QW[:, 0:8200].indirect(T.offD[:, eo + 8 * b0:eo + 8 * (b0 + m)])
+            x1, xw = c0 + x0, 128 * m
             if s < VS["D"][k]:
-                add([("V", TT, ((T.acc[:, c0:c0 + cw], src, (T.acc if s else T.Qs)[:, c0:c0 + cw], A.add), {}), gcost("V", cw))],
-                    QK + [("offD", k), ("acc", k), ("Qs", k)], [("acc", k)])
+                add([("V", TT, ((T.acc[:, x1:x1 + xw], src, (T.acc if s else T.Qs)[:, x1:x1 + xw], A.add), {}), gcost("V", xw))],
+                    QK + [("offD", k), ("acc", x1), ("Qs", k)], [("acc", x1)])
             else:
-                gather("S", T.GD[:, at:at + cw], src, cw, QK + [("offD", k)], [("GD", k, s)])
-                mm(T[b_][:, 0:cw], T.idf[:], T.GD[:, at:at + cw], s == VS["D"][k], s == 5, cw, True, [("GD", k, s), "idf"], [("qk", k)], b_)
-                at += cw
-        vec(TT, (T.Qs[:, c0:c0 + cw], T.acc[:, c0:c0 + cw], T[b_][:, 0:cw], A.add), cw, [("acc", k), ("qk", k)], [("Qs", k)], [b_])
+                if (s - VS["D"][k]) % 2 == 0:
+                    two = min(2, 6 - s)
+                    gather("S", T.GD[:, at:at + two * xw], T.QW[:, 0:8200].indirect(T.offD[:, eo + 8 * b0:eo + 8 * (b0 + two * m)]), two * xw,
+                           QK + [("offD", k)], [("GD", at + xw * i) for i in range(two)])
+                mm(T[b_][:, x0:x0 + xw], T.idf[:], T.GD[:, at:at + xw], s == VS["D"][k], s == 5, xw, True, [("GD", at), "idf"], [("qk", k)], b_)
+                at += xw
+        vec(TT, (T.Qs[:, c0:c0 + cw], T.acc[:, c0:c0 + cw], T[b_][:, 0:cw], A.add), cw, [("acc", c0), ("acc", c0 + 128), ("qk", k)],
+            [("Qs", k)], [b_])
         copy(T[b_][:, 0:cw], T.Qs[:, c0:c0 + cw], cw, [("Qs", k)], [("qk", k)], [b_])
         dma("Y", T.q1[:, c0:c0 + cw], T.Qs[:, c0:c0 + cw], 512 * cw, "do%d" % k, [("Qs", k)], [("q1", k)])
     QS = [("Qs", k) for k in KS]
@@ -459,7 +474,7 @@ def rank_program(g, core, T, topo):
         pure(k, "WB", "WF", "offE", "GA")
         mm(T[b_][:, 0:ne], T.idn[:], T.t2[:, eo:eo + ne], True, False, ne, False, ["idn", ("t2", k)], [("tk", k)], b_)
         mm(T[b_][:, 0:ne], T.bigi[:], T.ab[:, eo:eo + ne], False, False, ne, False, ["bigi", ("ab", k)], [("tk", k)], b_)
-        to_dense(k, "GA", range(6 * n), T.RB[:, 0:8], ["RB"], ne, False, True, False)
+        to_dense(k, "GA", blocks(k), T.RB[:, 0:8], ["RB"], ne, False, True, False)
         collapse(k, (0, 0), "X1")
         window(k, "WG", "sum")
     send("WG", 128, "WG", ("WG", 0), 4)

from concourse.bass import DstId, RemoteDMATransfer
from concourse.mybir import AluOpType, ActivationFunctionType

A = AluOpType
COPY = ActivationFunctionType.Copy
IDENT = ActivationFunctionType.Identity
NV = 1024
CH = [(0, 2), (2, 3), (5, 3)]
BIG = float(1 << 26)
RESET = float(1 << 29)
ZERO = 8192
VS = {"A": (2, 2, 2), "D": (4, 3, 3), "E": (1, 1, 2)}
PIECE = 4
NEMAX = 48 * max(n for _c, n in CH)
CYC, GAT, PEC, WAKE, DMAL, REML, FIRST, BW, LOOK, SHARE = 0.001, 1.56, 0.00055, 0.17, 2.0, 3.2, 2.0, 200000.0, 0.05, 0.3
PRI = {'D22S': -14.0, '021S': -7.5, 'W22V': 30.0, 'A21V': 1.5, 'B21V': -10.0, 'B11V': -0.5, 'W12V': 37.0, 'B12S': -14.0, 'B22V': 0.5,
       '011V': 11.0, 'E12S': -20.0, 'D02V': -13.5, 'W02V': 38.0, 'A02V': -13.5, 'D22V': 5.0, 'W02S': -5.5, 'E22S': 15.0, 'C12V': -9.0,
       'F21V': -26.5, 'F22V': -10.5, 'C01V': -1.0, 'B02S': 15.5, 'D01S': 7.0, 'D11S': -4.0, '021V': -1.5, 'W11S': -44.0, 'C21V': 2.5,
       'A22V': 41.5, 'W21S': 27.5, 'E22V': 27.0, 'F22S': -44.0, 'F02S': 3.0, 'F11V': -8.0, 'D02S': 4.5, 'D12S': 16.5, 'F01V': 3.5,
       'G22S': 7.0, 'W12S': -53.0, 'C12S': 3.5, 'A12V': -30.0, 'G21V': -6.0, 'W01S': -3.0, 'W11V': 7.5, 'E02S': -6.5, 'C22S': -3.0,
       '001V': 9.5, 'W22S': 18.5, 'F02V': 30.5, 'D12V': -55.0, 'B02V': 37.5, 'A22S': -7.5, 'G22V': -12.0, 'A12S': 18.0, 'A02S': 38.0,
       'W01V': -0.5, 'C02S': 2.5, 'B01V': 64.5, 'A01S': 10.5, 'A11S': 11.5, 'E01S': 1.0, 'B12V': 18.0, 'W21V': -0.5, 'G21S': -21.5,
       'F12S': -2.0, 'A01V': 3.5, 'C22V': -38.0, 'E21S': -22.0, 'A21S': -13.0, '001S': -7.5, 'F12V': -3.5, 'E02V': -8.5, 'D21S': 23.5,
       'E11V': 1.0, 'E12V': 11.0, 'A11V': 5.5, 'C11V': 4.0, 'C02V': -8.5, 'D01V': -1, 'B22S': -17.0, 'E11S': 2.0, 'E21V': -4.0}

SCRATCH = {"nb3": ("sbuf", [128, 6, 64], "int32"), "ci": ("sbuf", [128, 8], "int32")}
for _names, _cols, _dt in [
        ("W1 W2 WB WC", 8192, "bfloat16"), ("WG", 8192, "float32"), ("QW", 8200, "float32"),
        ("PR", 6144, "float32"), ("GD", 4096, "float32"), ("GA GB", 6144, "bfloat16"),
        ("Pn", 1024, "bfloat16"), ("Qs acc", 1024, "float32"),
        ("off1 offD offE", 384, "uint16"), ("offG", 64, "uint16"), ("nbz vL xL", 384, "float32"),
        ("vT Er Mn kp ids dl sc sd", 384, "float32"), ("tz", 768, "bfloat16"), ("t2 ab", 384, "bfloat16"),
        ("Es dch tm tn to", 64, "float32"),
        ("patR patK", NEMAX, "float32"), ("cf gi RA", 16, "float32"), ("RE", 8, "float32"), ("RB", 16, "bfloat16"),
        ("ones idn dbl bigi", 128, "bfloat16"), ("idf", 128, "float32"), ("sel", 144, "bfloat16")]:
    for _x in _names.split():
        SCRATCH[_x] = ("sbuf", [128, _cols], _dt)
for _k, (_c, _n) in enumerate(CH):
    SCRATCH["X1%d" % _k] = ("sbuf", [128, 8, 16 * _n], "bfloat16")
    SCRATCH["X2%d" % _k] = ("sbuf", [128, 8, 16 * _n], "bfloat16")
    SCRATCH["qk%d" % _k] = ("psum", [128, 512], "float32")
    SCRATCH["tk%d" % _k] = ("psum", [128, 512], "float32")
SCRATCH["wa0"] = ("psum", [128, 512], "float32")
SCRATCH["wa1"] = ("psum", [128, 512], "float32")

SENDS = ["Q", "W1", "WB", "WC", "W2", "WF", "WG"]
SEMAPHORES = (["cV", "cS", "cP", "cG", "dnb", "dgo"] + ["dq%d" % k for k in range(4)] + ["dp%d" % k for k in range(4)]
              + ["do%d" % k for k in range(3)] + ["df%d" % k for k in range(6)] + ["a" + x for x in SENDS] + ["l" + x for x in SENDS])


def arrange(ops):
    n = len(ops)
    writer, readers = {}, {}
    pred = [set() for _ in ops]
    for i, o in enumerate(ops):
        for k in o["r"]:
            if k in writer:
                pred[i].add(writer[k])
        for k in o["w"]:
            if k in writer:
                pred[i].add(writer[k])
            pred[i].update(readers.get(k, ()))
        pred[i].discard(i)
        for k in o["r"]:
            readers.setdefault(k, set()).add(i)
        for k in o["w"]:
            writer[k] = i
            readers[k] = set()
    succ = [[] for _ in ops]
    for i in range(n):
        for j in pred[i]:
            succ[j].append(i)
    tail = [0.0] * n
    for i in range(n - 1, -1, -1):
        o = ops[i]
        tail[i] = o["alt"][0][3] + o["lat"] + o["bytes"] / BW + WAKE + max([tail[j] for j in succ[i]] + [0.0]) + o["bump"]
    left = [len(p) for p in pred]
    ready = [i for i in range(n) if not left[i]]
    done, who = [0.0] * n, [None] * n
    free, bank, dma, first = {}, {}, [0.0], [FIRST]
    order = []

    def start(i, q):
        t = free.get(q, 0.0)
        for j in pred[i]:
            t = max(t, done[j] + (0.0 if q == "P" and who[j] == "P" else WAKE))
        for b in ops[i]["banks"]:
            for q2, t2 in bank.get(b, {}).items():
                if q2 != q:
                    t = max(t, t2 + WAKE)
        return t
    while ready:
        cand = [(start(i, a[0]), i, a) for i in ready for a in ops[i]["alt"]]
        st = {(i, a[0]): t for t, i, a in cand}
        cand = [c for c in cand if not (c[2][0] == "V" and st.get((c[1], "S"), 1e9) <= c[0] + SHARE)]
        t0, _i, a0 = min(cand, key=lambda c: (c[0], -tail[c[1]]))
        t, i, a = max((c for c in cand if c[2][0] == a0[0] and c[0] <= t0 + LOOK),
                      key=lambda c: (tail[c[1]] + PRI.get(ops[c[1]]["grp"] + c[2][0], 0.0), -c[1]))
        o = ops[i]
        q = a[0]
        free[q] = t + a[3]
        done[i] = t + a[3]
        if o["lat"]:
            lat = o["lat"]
            if o["remote"]:
                lat += first[0]
                first[0] = 0.0
            dma[0] = max(dma[0], t + lat) + o["bytes"] / BW
            done[i] = dma[0]
        who[i] = q
        for b in o["banks"]:
            bank.setdefault(b, {})[q] = done[i]
        order.append((i, a))
        ready.remove(i)
        for j in succ[i]:
            left[j] -= 1
            if not left[j]:
                ready.append(j)
    return order, pred, max(done)


def rank_program(g, core, T, topo):
    me = T.rank_of(core)
    if me is None:
        return
    V, S, P = g.vector, g.scalar, g.tensor
    queue = {"V": V, "S": S, "P": P, "G": g, "Y": g.sync}
    ops = []
    stage = ["0", "0"]

    def add(alt, r=(), w=(), banks=(), sem=None, inc=1, lat=0.0, nbytes=0, remote=None, bump=0.0):
        ops.append(dict(alt=alt, r=list(r), w=list(w), banks=list(banks), sem=sem, inc=inc, lat=lat, bytes=nbytes, remote=remote, bump=bump,
                        grp=stage[0] + stage[1] + ("2" if len(alt) > 1 else "1")))

    def vec(fn, args, n, r=(), w=(), banks=()):
        add([("V", fn, (args, {}), max(n, 64) * CYC)], r, w, banks)

    def act(out, in_, n, r=(), w=(), banks=(), **kw):
        add([("S", S.activation, ((out, in_, IDENT if "bias" in kw else COPY), kw), max(n, 64) * CYC)], r, w, banks)

    def copy(out, in_, n, r=(), w=(), banks=()):
        add([("S", S.activation, ((out, in_, COPY), {}), max(n, 64) * CYC), ("V", V.tensor_copy, ((out, in_), {}), max(n, 64) * CYC)], r, w, banks)

    def mm(out, lh, rh, start, stop, n, f32, r, w, b):
        add([("P", P.matmul, ((out, lh, rh, start, stop), {}), max(n, 64) * (4 if f32 else 1) * PEC)], r, list(w) + [("pe", b)], [b])

    def pool(fn, args, n, r=(), w=(), **kw):
        add([("G", fn, (args, kw), 0.17 + 2 * n * CYC)], r, w)

    def dma(q, out, in_, nbytes, sem, r=(), w=(), bump=0.0):
        add([(q, queue[q].dma_start, ((out, in_), {}), 0.1)], r, w, sem=sem, inc=16, lat=DMAL, nbytes=nbytes, bump=bump)

    def gcost(q, n):
        return (0.06 if q == "V" else 0.08) + n * GAT * CYC

    peers = [c for c in T.cores if c != core]
    mask = topo.mask(core, peers[0])
    for c in peers:
        mask &= topo.mask(core, c)
    neng = bin(mask).count("1")
    dsts = [DstId(rid=topo.addr(c)[0], pnc=topo.addr(c)[1]) for c in peers]
    own = NV * me

    def send(win, cols, name, key, size):
        ap = T[win][:, own:own + cols]
        tr = RemoteDMATransfer(dst_ids=dsts, dma_engine_mask=mask, remote_sem=T.sem["a" + name], srcs=[ap], dsts=[ap] * len(peers))
        add([("G", g.remote_dma_fused, (([tr],), {"local_sem": T.sem["l" + name]}), 0.3)], [key], [("halo", name)], sem="l" + name,
            inc=neng, lat=REML, nbytes=128 * cols * size * len(peers), remote="a" + name)

    def geo(k):
        cb, n = CH[k]
        stage[1] = str(k)
        return n, 128 * cb, 128 * n, 8 * cb, 8 * n, 48 * cb, 48 * n, 768 * cb

    KS = range(len(CH))
    TT, TS, CP, SCAN, MS = V.tensor_tensor, V.tensor_scalar, V.tensor_copy, V.tensor_tensor_scan, V.memset

    def quarters(c0, cw):
        return [("Q", j) for j in range(c0 // 256, (c0 + cw + 255) // 256)], [("Pn", j) for j in range(c0 // 256, (c0 + cw + 255) // 256)]

    for j in range(4):
        dma("Y", T.QW[:, own + 256 * j:own + 256 * j + 256], T.qu[:, 256 * j:256 * j + 256], 131072, "dq%d" % j, w=[("Q", j)], bump=4.0 - j)
        dma("S", T.Pn[:, 256 * j:256 * j + 256], T.po[:, 256 * j:256 * j + 256], 65536, "dp%d" % j, w=[("Pn", j)], bump=4.0 - j)
    dma("Y", T.nb3[:], T.nb[:], 196608, "dnb", w=["nb"])

    F = dict(allow_small_or_imprecise_dtypes=True)
    cf = T.cf
    jj, ii, pm, pg = cf[:, 0:1], cf[:, 1:2], cf[:, 2:3], cf[:, 3:4]
    sp, ns, we, idr, cw_, cb_, cc_ = (cf[:, i:i + 1] for i in range(4, 11))
    pool(g.iota, (T.ci[:, 0:1], [[0, 1]], 0, 1), 1, w=["ci0"])
    pool(g.iota, (T.gi[:], [[0, 2], [1, 8]], 0, 0), 16, w=["gi"], **F)
    vec(MS, (T.ones[:], 1.0), 64, w=["ones"])
    pool(g.affine_select, (T.idn[:], T.ones[:], [[-1, 128]], A.is_equal, 0.0, 0, 1), 128, r=["ones"], w=["idn"])
    vec(TS, (T.ci[:, 1:2], T.ci[:, 0:1], 3, None, A.bitwise_and), 1, ["ci0"], ["ci1"])
    vec(TS, (T.ci[:, 2:3], T.ci[:, 0:1], 2, 3, A.arith_shift_right, A.bitwise_and), 1, ["ci0"], ["ci2"])
    vec(TS, (T.ci[:, 3:4], T.ci[:, 0:1], 15, None, A.bitwise_and), 1, ["ci0"], ["ci3"])
    vec(TS, (T.ci[:, 4:5], T.ci[:, 0:1], 4, None, A.arith_shift_right), 1, ["ci0"], ["ci4"])
    vec(CP, (cf[:, 0:4], T.ci[:, 1:5]), 4, ["ci1", "ci2", "ci3", "ci4"], ["cf"])
    vec(TS, (sp, ii, jj, None, A.is_gt), 1, ["cf"], ["sp"])
    vec(TS, (ns, ii, jj, None, A.is_le), 1, ["cf"], ["ns"])
    vec(TS, (we, ii, jj, ns, A.is_lt, A.add), 1, ["cf", "ns"], ["we"])
    vec(TS, (T.RE[:], T.gi[:, 0:8], pg, we, A.is_equal, A.mult), 8, ["gi", "cf", "we"], ["RE"])
    vec(TS, (T.dbl[:], T.idn[:], we, None, A.mult), 64, ["idn", "we"], ["dbl"])
    vec(TS, (idr, pm, 12.0, sp, A.is_ge, A.mult), 1, ["cf", "sp"], ["idr"])
    vec(TS, (cb_, pm, 3.0, None, A.is_lt), 1, ["cf"], ["cb"])
    vec(TS, (cc_, pm, 14.0, None, A.is_ge), 1, ["cf"], ["cc"])
    vec(TS, (cw_, idr, -1.0, 1.0, A.mult, A.add), 1, ["idr"], ["cw"])
    vec(TS, (T.RA[:, 8:16], T.gi[:, 0:8], pg, idr, A.is_equal, A.mult), 8, ["gi", "cf", "idr"], ["RA1"])
    vec(MS, (T.sel[:], 0.0), 72, w=["sel"])
    vec(TS, (T.RB[:], T.gi[:], pg, cb_, A.is_equal, A.mult), 16, ["gi", "cf", "cb"], ["RB"])
    vec(TS, (T.RA[:, 0:8], T.gi[:, 0:8], pg, cw_, A.is_equal, A.mult), 8, ["gi", "cf", "cw"], ["RA0"])
    vec(TS, (T.sel[:, 15:143:16], T.gi[:, 0:8], pg, cc_, A.is_equal, A.mult), 8, ["gi", "cf", "cc"], ["sel"])
    vec(MS, (T.patR[:], 0.0), NEMAX, w=["patR"])
    vec(MS, (T.patK[:], 1.0), NEMAX, w=["patK"])
    vec(MS, (T.tz[:], 0.0), 384, w=[("tz", k) for k in KS])
    vec(MS, (T.patR[:, 0:NEMAX:6], RESET), 1, w=["patR"])
    vec(MS, (T.patK[:, 0:NEMAX:6], 0.0), 1, w=["patK"])
    vec(MS, (T.QW[:, ZERO:ZERO + 8], 0.0), 1, w=["qz"])
    vec(MS, (T.dl[:, 0:384:48], 0.0), 1, w=[("dl", k) for k in KS])
    act(T.bigi[:], T.idn[:], 128, ["idn"], ["bigi"], scale=BIG)
    act(T.idf[:], T.idn[:], 128, ["idn"], ["idf"])
    RC = T.sel[:, 15:143:16]
    for k in KS:
        n, c0, cw, vo, w, eo, ne, go = geo(k)
        X = T["X1%d" % k]
        vec(MS, (X[:], 0.0), 64 * n, w=[("X1", k)])
        pool(g.iota, (X[:, :, 12 * n:13 * n], [[0, 8], [128, n]], own + c0, 0), w, w=[("X1", k)], **F)
        pool(g.iota, (X[:, :, 13 * n:14 * n], [[0, 8], [0, n]], 0, 1), w, w=[("X1", k)], **F)
        pool(g.iota, (T.vT[:, eo:eo + ne], [[0, 8], [128, n], [0, 6]], own + c0, 1), ne, w=[("vT", k)], **F)
        pool(g.iota, (T["X2%d" % k][:], [[0, 8], [0, 16 * n]], 0, 0), 128 * n, w=[("X2", k)], **F)
        pool(g.iota, (T.vL[:, eo:eo + ne], [[0, 6], [16, w]] if k else [[128, 2], [0, 6], [16, 8]], own + c0, 0), ne, w=["vL"], **F)
        for e0, e1, v0, v1 in ([(eo, eo + ne, vo, vo + w)] if k else [(0, 48, 0, 8), (48, 96, 8, 16)]):
            vec(TS, (T.off1[:, e0:e1], T.nb3[:, :, v0:v1], float(-own if e0 else 0), None, A.add), e1 - e0, ["nb"], [("off1", k)])
            vec(TS, (T.nbz[:, e0:e1], T.nb3[:, :, v0:v1], float(-ZERO), None, A.add), e1 - e0, ["nb"], [("nbz", k)])
    act(T.vL[:], T.vL[:], 384, ["cf", "vL"], ["vL"], bias=pm)

    def digits3(k, src, rk, banks, X, xk, rows):
        n, c0, cw, vo, w, eo, ne, go = geo(k)
        h, m, lo = (X[:, :, r * n:(r + 1) * n] for r in rows)
        rem = T.tm[:, vo:vo + w]
        vec(CP, (h, src), w, rk, [xk], banks)
        vec(TT, (rem, src, h, A.subtract), 2 * w, rk + [xk], [("tm", k)], banks)
        vec(CP, (m, rem), w, [("tm", k)], [xk])
        vec(TT, (lo, rem, m, A.subtract), 2 * w, [("tm", k), xk], [xk])

    wturn = [0]

    def window(k, win, kind):
        n, c0, cw, vo, w, eo, ne, go = geo(k)
        b = "wa%d" % (wturn[0] % 2)
        wturn[0] += 1
        ps, X1, X2 = T[b], T["X1%d" % k], T["X2%d" % k]
        if kind == "P":
            mm(ps[:, 0:cw], T.dbl[:], T.Pn[:, c0:c0 + cw], True, False, cw, False, ["dbl"] + quarters(c0, cw)[1], [b], b)
            for j in range(n):
                mm(ps[:, 128 * j:128 * j + 128], X1[:, :, j:16 * n:n], T.idn[:], False, j == n - 1, 128, False, [("X1", k), "idn"], [b], b)
        else:
            for j in range(n):
                o = ps[:, 128 * j:128 * j + 128]
                mm(o, X2[:, :, j:16 * n:n], T.idn[:], True, kind != "sum", 128, False, [("X2", k), "idn"], [b], b)
                if kind == "sum":
                    mm(o, X1[:, :, j:16 * n:n], T.idn[:], False, True, 128, False, [("X1", k), "idn"], [b], b)
        copy(T[win][:, own + c0:own + c0 + cw], ps[:, 0:cw], cw, [b], [(win, k)], [b])

    def units(k):
        n = CH[k][1]
        return [(s, s * n, n, 0) for s in range(6)] if k else [(s, 6 * j + s, 1, 128 * j) for j in (1, 0) for s in range(6)]

    def view(win, halo, far):
        keys = [(win, j) for j in KS]
        if far:
            return T[win][:, 0:8192], keys + [("halo", halo)]
        return T[win][:, own:own + NV], keys

    def blocks(k):
        return [b for s, b0, m, x0 in units(k) for b in range(b0, b0 + m)]

    def gather(qs, dst, src, n, r, w):
        alt = {"V": ("V", CP, ((dst, src), {}), gcost("V", n)), "S": ("S", S.activation, ((dst, src, COPY), {}), gcost("S", n))}
        add([alt[q] for q in qs], r, w)

    def to_dense(k, buf, blocks, rhs, rk, width, first, last, f32):
        n, c0, cw, vo, w, eo, ne, go = geo(k)
        b_ = "tk%d" % k
        for i, b in enumerate(blocks):
            s, j = divmod(b, n) if k else (b % 6, b // 6)
            mm(T[b_][:, 6 * j + s:width:6 * n], T[buf][:, go + 128 * b:go + 128 * b + 128], rhs, first,
               first or (last and i == len(blocks) - 1), 16, f32, [(buf, k, b)] + rk, [("tk", k)], b_)

    def cost(k, name, win, off, gbuf, rhs, rk, width, first):
        n, c0, cw, vo, w, eo, ne, go = geo(k)
        for i, (s, b0, m, x0) in enumerate(units(k)):
            wv, wk = view(win, win, k == 0 and (x0 == 0 or off != "off1"))
            g0, g1, xw = go + 128 * b0, go + 128 * (b0 + m), 128 * m
            ks = [("PR", k, b) for b in range(b0, b0 + m)]
            src = wv.indirect(T[off][:, eo + 8 * b0:eo + 8 * (b0 + m)])
            if s < VS[name][k]:
                add([("V", TT, ((T.PR[:, g0:g1], src, T.Qs[:, c0 + x0:c0 + x0 + xw], A.mult), {}), gcost("V", xw))],
                    wk + [(off, k), ("Qs", k)], ks)
            else:
                gk = [(gbuf, k, b) for b in range(b0, b0 + m)]
                if (s - VS[name][k]) % 2 == 0:
                    b1 = b0 + m * min(2, 6 - s)
                    gather("S", T[gbuf][:, g0:go + 128 * b1], wv.indirect(T[off][:, eo + 8 * b0:eo + 8 * b1]), 128 * (b1 - b0),
                           wk + [(off, k)], [(gbuf, k, b) for b in range(b0, b1)])
                vec(TT, (T.PR[:, g0:g1], T[gbuf][:, g0:g1], T["qk%d" % k][:, x0:x0 + xw], A.mult), xw, gk + [("qk", k)], ks, ["qk%d" % k])
            to_dense(k, "PR", range(b0, b0 + m), rhs, rk, width, first, i == len(units(k)) - 1, True)

    def best(k):
        n, c0, cw, vo, w, eo, ne, go = geo(k)
        vec(SCAN, (T.Mn[:, eo:eo + ne], T.patR[:, 0:ne], T["tk%d" % k][:, 0:ne], 0.0, A.add, A.min), ne,
            ["patR", ("tk", k)], [("Mn", k)], ["tk%d" % k])
        digits3(k, T.Mn[:, eo + 5:eo + ne:6], [("Mn", k)], [], T["X2%d" % k], ("X2", k), (0, 1, 2))

    def steps(k, at):
        n, c0, cw, vo, w, eo, ne, go = geo(k)
        tk = T["tk%d" % k]
        copy(T.ids[:, eo:eo + ne], tk[:, at:at + ne], ne, [("tk", k)], [("ids", k)], ["tk%d" % k])
        vec(TT, (T.dl[:, eo + 1:eo + ne], T.ids[:, eo:eo + ne - 1], tk[:, at + 1:at + ne], A.subtract), ne,
            [("tk", k), ("ids", k)], [("dl", k)], ["tk%d" % k])
        vec(TT, (T.to[:, vo:vo + w], T.vT[:, eo:eo + ne:6], tk[:, at + 5:at + ne:6], A.subtract), w,
            [("tk", k), ("vT", k)], [("to", k)], ["tk%d" % k])

    def choice(k):
        n, c0, cw, vo, w, eo, ne, go = geo(k)
        tk = T["tk%d" % k]
        vec(TT, (T.kp[:, eo + 1:eo + ne], tk[:, 1:ne], T.Mn[:, eo:eo + ne - 1], A.is_ge), ne, [("tk", k), ("Mn", k)], [("kp", k)], ["tk%d" % k])
        add([("S", S.activation, ((T.kp[:, eo:eo + ne:6], T.vT[:, eo:eo + ne:6], COPY), {"scale": 0.0}), 64 * CYC),
             ("V", MS, ((T.kp[:, eo:eo + ne:6], 0.0), {}), 64 * CYC)], [("vT", k)], [("kp", k)])
        vec(SCAN, (T.sd[:, eo:eo + ne], T.dl[:, eo:eo + ne], T.kp[:, eo:eo + ne], 0.0, A.add, A.mult), ne, [("dl", k), ("kp", k)], [("sd", k)])
        vec(TT, (T.dch[:, vo:vo + w], T.sd[:, eo + 5:eo + ne:6], T.to[:, vo:vo + w], A.subtract), 2 * w, [("sd", k), ("to", k)], [("dch", k)])

    def collapse(k, rows, xl):
        n, c0, cw, vo, w, eo, ne, go = geo(k)
        tn, tm = T.tn[:, vo:vo + w], T.tm[:, vo:vo + w]
        h, lo = T["X2%d" % k][:, :, rows[0] * n:(rows[0] + 1) * n], T[xl + str(k)][:, :, rows[1] * n:(rows[1] + 1) * n]
        vec(SCAN, (T.sc[:, eo:eo + ne], T.patR[:, 0:ne], T["tk%d" % k][:, 0:ne], 0.0, A.add, A.min), ne,
            ["patR", ("tk", k)], [("sc", k)], ["tk%d" % k])
        vec(TT, (tn, T.sc[:, eo + 5:eo + ne:6], T.Mn[:, eo + 5:eo + ne:6], A.is_gt), 2 * w, [("sc", k), ("Mn", k)], [("tn", k)])
        vec(TT, (tm, tn, T.dch[:, vo:vo + w], A.mult), 2 * w, [("tn", k), ("dch", k)], [("tm", k)])
        vec(TT, (tn, tm, T.vT[:, eo:eo + ne:6], A.add), 2 * w, [("tm", k), ("vT", k)], [("tn", k)])
        vec(CP, (h, tn), w, [("tn", k)], [("X2", k)])
        vec(TT, (lo, tn, h, A.subtract), 2 * w, [("tn", k), ("X2", k)], [(xl, k)])

    def pure(k, win, halo, off, gbuf):
        n, c0, cw, vo, w, eo, ne, go = geo(k)
        for b0, b1 in ([(b, min(b + PIECE, 6 * n)) for b in range(0, 6 * n, PIECE)] if k else [(6, 9), (9, 12), (0, 3), (3, 6)]):
            wv, wk = view(win, halo, k == 0 and (b0 < 6 or off != "off1"))
            gather("SV", T[gbuf][:, go + 128 * b0:go + 128 * b1], wv.indirect(T[off][:, eo + 8 * b0:eo + 8 * b1]), 128 * (b1 - b0),
                   wk + [(off, k)], [(gbuf, k, b) for b in range(b0, b1)])

    stage[0] = "W"
    for k in KS:
        n, c0, cw, vo, w, eo, ne, go = geo(k)
        tk, qk = T["tk%d" % k], T["qk%d" % k]
        for h0 in range(0, cw, 256):
            h1 = min(h0 + 256, cw)
            qk_, pk_ = quarters(c0 + h0, h1 - h0)
            act(qk[:, h0:h1], T.QW[:, own + c0 + h0:own + c0 + h1], h1 - h0, qk_ + ["sp", "ns"], [("qk", k)], ["qk%d" % k], bias=sp, scale=ns)
            vec(TT, (T.PR[:, go + h0:go + h1], T.Pn[:, c0 + h0:c0 + h1], qk[:, h0:h1], A.mult), h1 - h0, pk_ + [("qk", k)],
                [("PR", k, b) for b in range(h0 // 128, h1 // 128)], ["qk%d" % k])
        for j in range(n):
            mm(tk[:, j:w:n], T.PR[:, go + 128 * j:go + 128 * j + 128], T.RE[:], True, True, 8, True, [("PR", k, j), "RE"], [("tk", k)], "tk%d" % k)
        digits3(k, tk[:, 0:w], [("tk", k)], ["tk%d" % k], T["X1%d" % k], ("X1", k), (4, 8, 9))
        copy(T.Es[:, vo:vo + w], tk[:, 0:w], w, [("tk", k)], [("Es", k)], ["tk%d" % k])
        window(k, "W1", "P")
        act(T.Qs[:, c0:c0 + cw], T.QW[:, own + c0:own + c0 + cw], cw, quarters(c0, cw)[0] + ["sp", "ns"], [("Qs", k)], bias=sp, scale=ns)
    for j in range(4):
        act(T.QW[:, own + 256 * j:own + 256 * j + 256], T.QW[:, own + 256 * j:own + 256 * j + 256], 256, [("Q", j), "ns"], [("Q", j)], scale=ns)
    send("W1", 128, "W1", ("W1", 0), 2)
    send("QW", 128, "Q", ("Q", 0), 4)
    for s in range(6):
        act(T.Er[:, s:384:6], T.Es[:], 64, [("Es", k) for k in KS], [("Er", s)], scale=-1.0)

    stage[0] = "A"
    for k in KS:
        n, c0, cw, vo, w, eo, ne, go = geo(k)
        cost(k, "A", "W1", "off1", "GA", T.RA[:], ["RA0", "RA1"], 2 * ne, True)
        best(k)
        window(k, "WB", "X")
        vec(TT, (T.tz[:, 2 * eo:2 * eo + ne], T.vT[:, eo:eo + ne], T["tk%d" % k][:, ne:2 * ne], A.is_lt), ne,
            [("vT", k), ("tk", k)], [("tz", k)], ["tk%d" % k])
        steps(k, ne)
        choice(k)
    send("WB", 128, "WB", ("WB", 0), 2)

    stage[0] = "B"
    for k in KS:
        n, c0, cw, vo, w, eo, ne, go = geo(k)
        b_ = "tk%d" % k
        pure(k, "WB", "WB", "off1", "GB")
        mm(T[b_][:, 0:2 * ne], T.idn[:], T.tz[:, 2 * eo:2 * eo + 2 * ne], True, False, 2 * ne, False, ["idn", ("tz", k)], [("tk", k)], b_)
        mm(T[b_][:, ne:2 * ne], T.idf[:], T.Er[:, eo:eo + ne], False, False, ne, True, ["idf"] + [("Er", s) for s in range(6)], [("tk", k)], b_)
        to_dense(k, "GB", blocks(k), T.RB[:], ["RB"], 2 * ne, False, True, False)
        collapse(k, (14, 15), "X2")
        window(k, "WC", "X")
    send("WC", 128, "WC", ("WC", 0), 2)

    stage[0] = "C"
    for k in KS:
        n, c0, cw, vo, w, eo, ne, go = geo(k)
        b_ = lb = "tk%d" % k
        tk = T[b_]
        L = tk[:, 2 * ne:3 * ne]
        pure(k, "WC", "WC", "off1", "GA")
        to_dense(k, "GA", blocks(k), RC, ["sel"], ne, True, True, False)
        for r in range(16):
            mm(L, T.sel[:, 15 - r:143 - r], T.GA[:, go + r:go + 6 * cw:16], r == 0, r == 15, ne, False,
               [("GA", k, b) for b in range(6 * n)] + ["sel"], [("L", k)], lb)
        vec(TS, (T.offE[:, eo:eo + ne], L, float(-own if k else 0), None, A.add), ne, [("L", k)], [("offE", k)], [lb])
        vec(TT, (L, L, T.vL[:, eo:eo + ne], A.is_equal), ne, [("L", k), "vL"], [("L", k)], [lb])
        vec(TT, (T.xL[:, eo:eo + ne], L, T.nbz[:, eo:eo + ne], A.mult), ne, [("L", k), ("nbz", k)], [("xL", k)], [lb])
        vec(TS, (T.offD[:, eo:eo + ne], T.xL[:, eo:eo + ne], float(ZERO), None, A.add), ne, [("xL", k)], [("offD", k)])
        vec(TT, (T.ab[:, eo:eo + ne], tk[:, 0:ne], T.vT[:, eo:eo + ne], A.is_equal), ne, [("tk", k), ("vT", k)], [("ab", k)], [b_])
        vec(TT, (T.kp[:, eo:eo + ne], T.ab[:, eo:eo + ne], tk[:, ne:2 * ne], A.mult), ne, [("ab", k), ("tk", k)], [("kp", k)], [b_])
        vec(SCAN, (T.sc[:, eo:eo + ne], T.patK[:, 0:ne], T.kp[:, eo:eo + ne], 0.0, A.mult, A.add), ne, ["patK", ("kp", k)], [("sc", k)])
        vec(TT, (T.tn[:, vo:vo + w], T.sc[:, eo + 5:eo + ne:6], T.Es[:, vo:vo + w], A.add), 2 * w, [("sc", k), ("Es", k)], [("tn", k)])
        digits3(k, T.tn[:, vo:vo + w], [("tn", k)], [], T["X1%d" % k], ("X1", k), (4, 8, 9))
        window(k, "W2", "P")
        vec(TT, (T.t2[:, eo:eo + ne], T.vT[:, eo:eo + ne], tk[:, 0:ne], A.is_lt), ne, [("vT", k), ("tk", k)], [("t2", k)], [b_])
        steps(k, 0)
    send("W2", 256, "W2", ("W2", 0), 2)

    stage[0] = "D"
    QK = [("Q", j) for j in range(4)] + [("halo", "Q"), "qz"]
    at = 0
    for k in KS:
        n, c0, cw, vo, w, eo, ne, go = geo(k)
        b_ = "qk%d" % k
        for s, b0, m, x0 in units(k):
            src = T.QW[:, 0:8200].indirect(T.offD[:, eo + 8 * b0:eo + 8 * (b0 + m)])
            x1, xw = c0 + x0, 128 * m
            if s < VS["D"][k]:
                add([("V", TT, ((T.acc[:, x1:x1 + xw], src, (T.acc if s else T.Qs)[:, x1:x1 + xw], A.add), {}), gcost("V", xw))],
                    QK + [("offD", k), ("acc", x1), ("Qs", k)], [("acc", x1)])
            else:
                if (s - VS["D"][k]) % 2 == 0:
                    two = min(2, 6 - s)
                    gather("S", T.GD[:, at:at + two * xw], T.QW[:, 0:8200].indirect(T.offD[:, eo + 8 * b0:eo + 8 * (b0 + two * m)]), two * xw,
                           QK + [("offD", k)], [("GD", at + xw * i) for i in range(two)])
                mm(T[b_][:, x0:x0 + xw], T.idf[:], T.GD[:, at:at + xw], s == VS["D"][k], s == 5, xw, True, [("GD", at), "idf"], [("qk", k)], b_)
                at += xw
        vec(TT, (T.Qs[:, c0:c0 + cw], T.acc[:, c0:c0 + cw], T[b_][:, 0:cw], A.add), cw, [("acc", c0), ("acc", c0 + 128), ("qk", k)],
            [("Qs", k)], [b_])
        copy(T[b_][:, 0:cw], T.Qs[:, c0:c0 + cw], cw, [("Qs", k)], [("qk", k)], [b_])
        dma("Y", T.q1[:, c0:c0 + cw], T.Qs[:, c0:c0 + cw], 512 * cw, "do%d" % k, [("Qs", k)], [("q1", k)])
    QS = [("Qs", k) for k in KS]

    stage[0] = "E"
    for k in KS:
        n, c0, cw, vo, w, eo, ne, go = geo(k)
        b_ = "tk%d" % k
        mm(T[b_][:, 0:ne], T.bigi[:], T.ab[:, eo:eo + ne], True, False, ne, False, ["bigi", ("ab", k)], [("tk", k)], b_)
        cost(k, "E", "W2", "offE", "GB", T.RA[:, 0:8], ["RA0"], ne, False)
        if k == 0:
            for r in range(16):
                mm(T.wa1[:, 0:64], T.sel[:, 15 - r:143 - r], T.WC[:, own + r:own + NV:16], r == 0, r == 15, 64, False,
                   [("WC", j) for j in KS] + ["sel"], ["wa1"], "wa1")
            vec(CP, (T.offG[:, 0:8], T.wa1[:, 0:8]), 8, ["wa1"], ["offG0"], ["wa1"])
            vec(TS, (T.offG[:, 8:64], T.wa1[:, 8:64], float(-own), None, A.add), 56, ["wa1"], ["offG1"], ["wa1"])
            wturn[0] = 0
        best(k)
        window(k, "WB", "X")
        choice(k)
    send("WB", 256, "WF", ("WB", 0), 2)
    for i, (a, b) in enumerate((a, b) for a in range(4) for b in range(a)):
        dma("Y", T.q1[4 * a + b:128:16, :], T.Qs[4 * b + a:128:16, :], 32768, "df%d" % i,
            QS + [("q1", k) for k in KS] + [("halo", "WF")], [("q1f", i)])

    stage[0] = "F"
    for k in KS:
        n, c0, cw, vo, w, eo, ne, go = geo(k)
        b_ = "tk%d" % k
        pure(k, "WB", "WF", "offE", "GA")
        mm(T[b_][:, 0:ne], T.idn[:], T.t2[:, eo:eo + ne], True, False, ne, False, ["idn", ("t2", k)], [("tk", k)], b_)
        mm(T[b_][:, 0:ne], T.bigi[:], T.ab[:, eo:eo + ne], False, False, ne, False, ["bigi", ("ab", k)], [("tk", k)], b_)
        to_dense(k, "GA", blocks(k), T.RB[:, 0:8], ["RB"], ne, False, True, False)
        collapse(k, (0, 0), "X1")
        window(k, "WG", "sum")
    send("WG", 128, "WG", ("WG", 0), 4)

    stage[0] = "G"
    GK = [("WG", k) for k in KS] + QS
    gather("V", T.acc[:, 128:576], T.WG[:, own:own + NV].indirect(T.offG[:, 8:36]), 448, GK + ["offG1"], ["g1"])
    gather("S", T.acc[:, 576:1024], T.WG[:, own:own + NV].indirect(T.offG[:, 36:64]), 448, GK + ["offG1"], ["g2"])
    gather("VS", T.acc[:, 0:128], T.WG[:, 0:8192].indirect(T.offG[:, 0:8]), 128, GK + [("halo", "WG"), "offG0"], ["g0"])
    dma("Y", T.goal[:], T.acc[0:128:16, :], 32768, "dgo", ["g0", "g1", "g2"])

    order, pred, _t = arrange(ops)
    count, waited, mark, bank = {}, {}, {}, {}

    def wait(q, sem, val):
        if waited.get((q, sem), 0) < val:
            queue[q].wait_ge(T.sem[sem], val)
            waited[(q, sem)] = val

    for i, (q, fn, (args, kw), _c) in order:
        o = ops[i]
        need = {}
        marks = [t for j in pred[i] for t in mark[j]] + [t for b in o["banks"] for q2, t in bank.get(b, {}).items() if q2 != q]
        for sem, val in marks:
            if not (q == "P" and sem == "cP"):
                need[sem] = max(need.get(sem, 0), val)
        for sem, val in need.items():
            wait(q, sem, val)
        ins = fn(*args, **kw)
        sem = o["sem"] or "c" + q
        count[sem] = count.get(sem, 0) + o["inc"]
        mark[i] = [(sem, count[sem])]
        if o["remote"]:
            count[o["remote"]] = neng * len(peers)
            mark[i].append((o["remote"], count[o["remote"]]))
        else:
            ins.then_inc(T.sem[sem], o["inc"])
        for b in o["banks"]:
            bank.setdefault(b, {})[q] = mark[i][0]
    for sem, val in count.items():
        wait("Y" if sem in ("dgo", "cV", "cS") else "G", sem, val)
